import numpy as np
import ml_dtypes


def mxq(x, axis, fmt="e4m3"):
    dtype, down = {"e4m3": (ml_dtypes.float8_e4m3fn, 7), "e5m2": (ml_dtypes.float8_e5m2, 14)}[fmt]
    v = np.moveaxis(np.asarray(x, np.float32).astype(ml_dtypes.bfloat16).astype(np.float64), axis, -1)
    blocks = v.reshape(v.shape[:-1] + (-1, 32))
    amax = np.abs(blocks).max(-1, keepdims=True)
    byte = np.maximum(np.where(amax > 0, np.frexp(amax)[1] - 1 + 127, 0) - down, 1)
    scale = np.exp2(byte - 127.0)
    codes = (blocks / scale).astype(np.float32).astype(dtype).astype(np.float64)
    return np.moveaxis((codes * scale).reshape(v.shape), -1, axis)


WIDE = False


def mx_kscale(k):
    if not WIDE:
        return np.ones(k)
    levels = np.array([10, -10, 5, -5, 0])
    if k % 512:
        return np.exp2(np.random.permutation(np.resize(levels, k // 32))).repeat(32)
    a = np.empty((k // 512, 16))
    for p in range(k // 512):
        a[p, :8] = np.random.permutation(np.resize(levels, 8))
        for g in range(8):
            far = levels[np.abs(levels - a[p, g]) >= 10]
            a[p, g + 8] = far[np.random.randint(len(far))]
    return np.exp2(a.ravel()).repeat(32)


def f64(x):
    return np.asarray(x).astype(np.float64)


def striped(idx):
    return np.tile(idx.reshape(-1, 16).T, (8, 1)).astype(np.uint16)


def unstriped(offs):
    return offs[:16].T.reshape(-1).astype(np.int64)


def pack_weight(w):
    k, n = w.shape
    w = f64(np.asarray(w, np.float32).astype(ml_dtypes.bfloat16)).reshape(k // 32, 32, n)
    amax = np.abs(w).max(1)
    byte = np.clip(np.where(amax > 0, np.frexp(amax)[1] - 1 + 127 - 7, 1), 1, 254)
    scaled = (w * np.exp2(127.0 - byte)[:, None, :]).reshape(k, n).astype(np.float32)
    words = np.ascontiguousarray(scaled.reshape(k // 512, 128, 4, n).transpose(0, 1, 3, 2)).astype(ml_dtypes.float8_e4m3fn).view(np.uint8)
    return words, np.ascontiguousarray(byte.astype(np.uint8).reshape(k // 512, 16, n))


def unpack_weight(words, scales):
    g, p, n, _ = words.shape
    vals = np.ascontiguousarray(words).view(ml_dtypes.float8_e4m3fn).astype(np.float64) * np.repeat(np.exp2(scales.astype(np.float64) - 127.0), 8, axis=1)[..., None]
    return vals.transpose(0, 1, 3, 2).reshape(g * 512, n)


K, T, S, H, V, W = 1024, 2048, 512, 512, 512, 2048
P = 2 ** 7


def setup_inputs():
    n = np.random.standard_normal
    s = mx_kscale(K)[:, None]
    u = mx_kscale(H)
    packed_xT = pack_weight(n((K, T)) * s)
    packed_eT = pack_weight(n((H, W)) / np.sqrt(H) / u[:, None])
    return {
        "x_words": packed_xT[0],
        "x_scales": packed_xT[1],
        "w1": (n((K, H)) / np.sqrt(K) / s * u).astype(np.float32),
        "e_words": packed_eT[0],
        "e_scales": packed_eT[1],
        "inv": (np.tile(np.random.uniform(0.5, 2.0, W), (P, 1))).astype(np.float32),
        "offs": striped(np.random.permutation(T)[:S]),
        "pro": striped(np.random.permutation(W)[:V]),
    }


def reference(x_words, x_scales, w1, e_words, e_scales, inv, offs, pro):
    xq = unpack_weight(x_words, x_scales)[:, unstriped(offs)]
    h = mxq(f64(w1), 0, "e4m3").T @ xq
    e_pro = unpack_weight(e_words, e_scales)[:, unstriped(pro)]
    y = mxq(h, 0, "e4m3").T @ e_pro
    z = y * (f64(inv)[:1][:, unstriped(pro)])
    ex = np.exp(z - z.max(axis=1, keepdims=True))
    return ex / ex.sum(axis=1, keepdims=True)

@@ -1,0 +1,160 @@
+from contextlib import ExitStack
+
+import concourse.mybir as mybir
+from concourse.masks import make_identity
+
+F32 = mybir.dt.float32
+BF16 = mybir.dt.bfloat16
+I32 = mybir.dt.int32
+U32 = mybir.dt.uint32
+U16 = mybir.dt.uint16
+U8 = mybir.dt.uint8
+FP8X4 = mybir.dt.float8_e4m3fn_x4
+ALU = mybir.AluOpType
+ACT = mybir.ActivationFunctionType
+AX = mybir.AxisListType
+
+P = 128
+K, T, S, H, V, W = 1024, 2048, 512, 512, 512, 2048
+PASSES = K // 512
+TILES = S // P
+E_ROW = 8
+
+FLOPS = 2 * K * H * S + 2 * H * S * V
+
+
+def tile_picked_yphi_soft_p_kernel(tc, x_words, x_scales, w1, e_words, e_scales, inv, offs, pro, out):
+    nc = tc.nc
+    with ExitStack() as ctx:
+        keep = ctx.enter_context(tc.tile_pool(name="keep", bufs=1))
+        psum = ctx.enter_context(tc.psum_pool(name="psum", bufs=1))
+
+        offs_t = keep.tile([P, S // 16], U16, name="offs_t")
+        pro_t = keep.tile([P, V // 16], U16, name="pro_t")
+        w_raw = [keep.tile([P, 4, H], F32, name="w_raw%d" % o) for o in range(PASSES)]
+        x_tab = [keep.tile([P, T], I32, name="x_tab%d" % o) for o in range(PASSES)]
+        e_tab = keep.tile([P, W], I32, name="e_tab")
+        xs_tab = keep.tile([P, T], U8, name="xs_tab")
+        es_tab = keep.tile([P, W], U8, name="es_tab")
+        inv_tab = keep.tile([P, W], F32, name="inv_tab")
+        ident = keep.tile([P, P], F32, name="ident")
+        warm = keep.tile([P, 8], F32, name="warm")
+
+        nc.vector.memset(warm[:], 0.0)
+        nc.scalar.activation(warm[:, 1:2], warm[:, 0:1], ACT.Exp)
+
+        nc.sync.dma_start(w_raw[0][:], w1[0:512, :].rearrange("(p j) c -> p j c", j=4))
+        nc.sync.dma_start(offs_t[:], offs)
+        nc.sync.dma_start(pro_t[:], pro)
+        nc.sync.dma_start(inv_tab[P - 1 : P, :], inv[0:1, :])
+        nc.sync.dma_start(w_raw[1][:], w1[512:1024, :].rearrange("(p j) c -> p j c", j=4))
+        for o in range(PASSES):
+            nc.sync.dma_start(x_tab[o][:], x_words[o].rearrange("p n t -> p (n t)").bitcast(I32))
+        nc.sync.dma_start(e_tab[:], e_words[0].rearrange("p n t -> p (n t)").bitcast(I32))
+
+        make_identity(nc, ident[:])
+        nc.vector.memset(xs_tab[:].bitcast(I32), 0)
+        nc.vector.memset(es_tab[:].bitcast(I32), 0)
+        nc.vector.memset(inv_tab[0 : P - 1, :], 0.0)
+        for q in range(4):
+            nc.gpsimd.dma_start(xs_tab[32 * q : 32 * q + 8, :].bitcast(I32), x_scales[:, 4 * q : 4 * q + 4, :].bitcast(I32))
+        for q in range(4):
+            nc.gpsimd.dma_start(es_tab[32 * q + E_ROW : 32 * q + E_ROW + 4, :].bitcast(I32), e_scales[0, 4 * q : 4 * q + 4, :].bitcast(I32))
+
+        wq = keep.tile([P, PASSES, H], U32, name="wq", align_bytes=64)
+        ws = keep.tile([P, PASSES, H], U8, name="ws", align_bytes=64)
+        w_bf = [keep.tile([P, 4 * H], BF16, name="w_bf%d" % o, align_bytes=64) for o in range(PASSES)]
+
+        def cast_w(o):
+            nc.scalar.copy(
+                w_bf[o][:].rearrange("p (t m j) -> p m j t", t=4, j=4),
+                w_raw[o][:].rearrange("p j (m t) -> p m j t", t=4),
+            )
+
+        def quant_w(o):
+            nc.vector.quantize_mx(out=wq[:, o, :].bitcast(FP8X4), scales=ws[:, o, :], in_=w_bf[o][:])
+
+        cast_w(0)
+
+        inv_g = keep.tile([P, V], F32, name="inv_g")
+        nc.vector.tensor_copy(inv_g[:], inv_tab[:].indirect(pro_t[:]))
+        xs_g = keep.tile([P, S], U8, name="xs_g", align_bytes=64)
+        nc.vector.tensor_copy(xs_g[:], xs_tab[:].indirect(offs_t[:]))
+        quant_w(0)
+        cast_w(1)
+
+        turned = psum.tile([P, 4, P], F32, name="turned", tag="y0")
+        for b in range(4):
+            nc.tensor.transpose(turned[:, b, :], inv_g[:, b * P : (b + 1) * P], ident[:])
+        inv_col = keep.tile([P, 4], F32, name="inv_col")
+        nc.scalar.copy(inv_col[:], turned[:, :, P - 1])
+        spread = psum.tile([P, V], F32, name="spread", tag="y1")
+        for b in range(4):
+            nc.tensor.transpose(spread[:, b * P : (b + 1) * P], inv_col[:, b : b + 1].to_broadcast([P, P]), ident[:])
+        inv_b = keep.tile([P, V], F32, name="inv_b")
+        nc.scalar.copy(inv_b[:], spread[:])
+
+        es_g = keep.tile([P, V], U8, name="es_g", align_bytes=64)
+        nc.vector.tensor_copy(es_g[:], es_tab[:].indirect(pro_t[:]))
+
+        x_g = [keep.tile([P, S], U32, name="x_g%d" % o, align_bytes=64) for o in range(PASSES)]
+        nc.vector.tensor_copy(x_g[0][:], x_tab[0][:].bitcast(U32).indirect(offs_t[:]))
+        quant_w(1)
+        for half in range(2):
+            nc.vector.tensor_copy(x_g[1][:, 256 * half : 256 * (half + 1)], x_tab[1][:].bitcast(U32).indirect(offs_t[:, 16 * half : 16 * (half + 1)]))
+
+        hq = [keep.tile([P, P], U32, name="hq%d" % i, align_bytes=64) for i in range(TILES)]
+        hs = [keep.tile([P, P], U8, name="hs%d" % i, align_bytes=64) for i in range(TILES)]
+        h_bf = [keep.tile([P, P, 4], BF16, name="h_bf%d" % i, align_bytes=64) for i in range(TILES)]
+        for i in range(TILES):
+            cols = slice(i * P, (i + 1) * P)
+            acc = psum.tile([P, 4, P], F32, name="h%d" % i)
+            for t in range(4):
+                wc = slice(t * P, (t + 1) * P)
+                for o in range(PASSES):
+                    nc.tensor.matmul_mx(
+                        out=acc[:, t, :],
+                        lhsT=wq[:, o, wc].bitcast(FP8X4),
+                        lhsT_scale=ws[:, o, wc],
+                        rhs=x_g[o][:, cols].bitcast(FP8X4),
+                        rhs_scale=xs_g[4 * o : P, cols],
+                        start=(o == 0),
+                        stop=(o == PASSES - 1),
+                    )
+            nc.scalar.copy(h_bf[i][:], acc[:].rearrange("p t n -> p n t"))
+
+        def quant_h(i):
+            nc.vector.quantize_mx(out=hq[i][:].bitcast(FP8X4), scales=hs[i][:], in_=h_bf[i][:].rearrange("p n t -> p (n t)"))
+
+        e_g = keep.tile([P, V], U32, name="e_g", align_bytes=64)
+        quant_h(0)
+        nc.vector.tensor_copy(e_g[:], e_tab[:].bitcast(U32).indirect(pro_t[:]))
+        for i in range(1, TILES):
+            quant_h(i)
+
+        for i in range(TILES):
+            y = psum.tile([P, V], F32, name="y%d" % i, tag="y%d" % i)
+            nc.tensor.matmul_mx(
+                out=y[:],
+                lhsT=hq[i][:].bitcast(FP8X4),
+                lhsT_scale=hs[i][:],
+                rhs=e_g[:].bitcast(FP8X4),
+                rhs_scale=es_g[E_ROW:P, :],
+                start=True,
+                stop=True,
+            )
+            z = keep.tile([P, V], F32, name="z%d" % i)
+            neg_max = keep.tile([P, 1], F32, name="neg_max%d" % i)
+            total = keep.tile([P, 1], F32, name="total%d" % i)
+            recip = keep.tile([P, 1], F32, name="recip%d" % i)
+            ex = keep.tile([P, V], F32, name="ex%d" % i)
+            res = keep.tile([P, V], F32, name="res%d" % i)
+            nc.vector.tensor_tensor(z[:], y[:], inv_b[:], ALU.mult)
+            nc.vector.tensor_reduce(neg_max[:], z[:], AX.X, ALU.max, negate=True)
+            nc.scalar.activation(ex[:], z[:], ACT.Exp, bias=neg_max[:], accum_out=total[:])
+            nc.vector.reciprocal(recip[:], total[:])
+            if i < TILES - 1:
+                nc.scalar.activation(res[:], ex[:], ACT.Copy, scale=recip[:])
+            else:
+                nc.vector.tensor_scalar(res[:], ex[:], recip[:], None, ALU.mult)
+            nc.sync.dma_start(out[i * P : (i + 1) * P, :], res[:])

@@ -19,6 +19,7 @@ K, T, S, H, V, W = 1024, 2048, 512, 512, 512, 2048
 PASSES = K // 512
 TILES = S // P
 E_ROW = 8
+WARM = 3
 
 FLOPS = 2 * K * H * S + 2 * H * S * V
 
@@ -31,38 +32,52 @@ def tile_picked_yphi_soft_p_kernel(tc, x_words, x_scales, w1, e_words, e_scales,
 
         offs_t = keep.tile([P, S // 16], U16, name="offs_t")
         pro_t = keep.tile([P, V // 16], U16, name="pro_t")
-        w_raw = [keep.tile([P, 4, H], F32, name="w_raw%d" % o) for o in range(PASSES)]
+        w_raw = [keep.tile([P, 4, H], F32, name="w_raw%d" % o, tag="w_raw%d" % o) for o in range(PASSES)]
         x_tab = [keep.tile([P, T], I32, name="x_tab%d" % o) for o in range(PASSES)]
-        e_tab = keep.tile([P, W], I32, name="e_tab")
+        e_tab = keep.tile([P, W], I32, name="e_tab", tag="e_tab", align_bytes=64)
         xs_tab = keep.tile([P, T], U8, name="xs_tab")
-        es_tab = keep.tile([P, W], U8, name="es_tab")
+        es_tab = keep.tile([P, W], U8, name="es_tab", tag="es_tab", align_bytes=64)
         inv_tab = keep.tile([P, W], F32, name="inv_tab")
         ident = keep.tile([P, P], F32, name="ident")
         warm = keep.tile([P, 8], F32, name="warm")
 
+        nc.gpsimd.memset(xs_tab[:].bitcast(I32), 0)
+        nc.vector.memset(es_tab[:].bitcast(I32), 0)
         nc.vector.memset(warm[:], 0.0)
         nc.scalar.activation(warm[:, 1:2], warm[:, 0:1], ACT.Exp)
+        nc.vector.memset(inv_tab[0 : P - 1, :], 0.0)
+        make_identity(nc, ident[:])
 
-        nc.sync.dma_start(w_raw[0][:], w1[0:512, :].rearrange("(p j) c -> p j c", j=4))
-        nc.sync.dma_start(offs_t[:], offs)
-        nc.sync.dma_start(pro_t[:], pro)
-        nc.sync.dma_start(inv_tab[P - 1 : P, :], inv[0:1, :])
-        nc.sync.dma_start(w_raw[1][:], w1[512:1024, :].rearrange("(p j) c -> p j c", j=4))
-        for o in range(PASSES):
+        def load_w(o):
+            nc.sync.dma_start(w_raw[o][:], w1[512 * o : 512 * (o + 1), :].rearrange("(p j) c -> p j c", j=4))
+
+        def load_x(o):
             nc.sync.dma_start(x_tab[o][:], x_words[o].rearrange("p n t -> p (n t)").bitcast(I32))
+
+        def load_xs(n):
+            o, q = divmod(n, 4)
+            nc.sync.dma_start(xs_tab[32 * q + 4 * o : 32 * q + 4 * o + 4, :].bitcast(I32), x_scales[o, 4 * q : 4 * q + 4, :].bitcast(I32))
+
+        def load_es(q):
+            nc.sync.dma_start(es_tab[32 * q + E_ROW : 32 * q + E_ROW + 4, :].bitcast(I32), e_scales[0, 4 * q : 4 * q + 4, :].bitcast(I32))
+
+        nc.scalar.dma_start(inv_tab[P - 1 : P, :], inv[0:1, :])
+        nc.sync.dma_start(pro_t[:], pro)
+        nc.sync.dma_start(offs_t[:], offs)
+        load_w(0)
+        for n in range(6):
+            load_xs(n)
+        load_w(1)
+        for n in range(6, 8):
+            load_xs(n)
+        for q in range(4):
+            load_es(q)
+        load_x(0)
+        load_x(1)
         nc.sync.dma_start(e_tab[:], e_words[0].rearrange("p n t -> p (n t)").bitcast(I32))
 
-        make_identity(nc, ident[:])
-        nc.vector.memset(xs_tab[:].bitcast(I32), 0)
-        nc.vector.memset(es_tab[:].bitcast(I32), 0)
-        nc.vector.memset(inv_tab[0 : P - 1, :], 0.0)
-        for q in range(4):
-            nc.gpsimd.dma_start(xs_tab[32 * q : 32 * q + 8, :].bitcast(I32), x_scales[:, 4 * q : 4 * q + 4, :].bitcast(I32))
-        for q in range(4):
-            nc.gpsimd.dma_start(es_tab[32 * q + E_ROW : 32 * q + E_ROW + 4, :].bitcast(I32), e_scales[0, 4 * q : 4 * q + 4, :].bitcast(I32))
-
-        wq = keep.tile([P, PASSES, H], U32, name="wq", align_bytes=64)
-        ws = keep.tile([P, PASSES, H], U8, name="ws", align_bytes=64)
+        wq = {}
+        ws = [keep.tile([P, H], U8, name="ws%d" % o, align_bytes=64) for o in range(PASSES)]
         w_bf = [keep.tile([P, 4 * H], BF16, name="w_bf%d" % o, align_bytes=64) for o in range(PASSES)]
 
         def cast_w(o):
@@ -72,89 +87,117 @@ def tile_picked_yphi_soft_p_kernel(tc, x_words, x_scales, w1, e_words, e_scales,
             )
 
         def quant_w(o):
-            nc.vector.quantize_mx(out=wq[:, o, :].bitcast(FP8X4), scales=ws[:, o, :], in_=w_bf[o][:])
+            wq[o] = keep.tile([P, H], U32, name="wq%d" % o, tag=("wq0", "es_tab")[o], align_bytes=64)
+            nc.vector.quantize_mx(out=wq[o][:].bitcast(FP8X4), scales=ws[o][:], in_=w_bf[o][:])
 
         cast_w(0)
+        cast_w(1)
 
         inv_g = keep.tile([P, V], F32, name="inv_g")
         nc.vector.tensor_copy(inv_g[:], inv_tab[:].indirect(pro_t[:]))
-        xs_g = keep.tile([P, S], U8, name="xs_g", align_bytes=64)
-        nc.vector.tensor_copy(xs_g[:], xs_tab[:].indirect(offs_t[:]))
-        quant_w(0)
-        cast_w(1)
-
         turned = psum.tile([P, 4, P], F32, name="turned", tag="y0")
         for b in range(4):
             nc.tensor.transpose(turned[:, b, :], inv_g[:, b * P : (b + 1) * P], ident[:])
-        inv_col = keep.tile([P, 4], F32, name="inv_col")
+        inv_col = keep.tile([P, 4], F32, name="inv_col", tag="w_raw1")
         nc.scalar.copy(inv_col[:], turned[:, :, P - 1])
+        quant_w(0)
         spread = psum.tile([P, V], F32, name="spread", tag="y1")
         for b in range(4):
             nc.tensor.transpose(spread[:, b * P : (b + 1) * P], inv_col[:, b : b + 1].to_broadcast([P, P]), ident[:])
         inv_b = keep.tile([P, V], F32, name="inv_b")
         nc.scalar.copy(inv_b[:], spread[:])
 
+        xs_g = keep.tile([P, S], U8, name="xs_g", align_bytes=64)
+        nc.vector.tensor_copy(xs_g[:], xs_tab[:].indirect(offs_t[:]))
         es_g = keep.tile([P, V], U8, name="es_g", align_bytes=64)
         nc.vector.tensor_copy(es_g[:], es_tab[:].indirect(pro_t[:]))
-
-        x_g = [keep.tile([P, S], U32, name="x_g%d" % o, align_bytes=64) for o in range(PASSES)]
-        nc.vector.tensor_copy(x_g[0][:], x_tab[0][:].bitcast(U32).indirect(offs_t[:]))
         quant_w(1)
+        x_first = keep.tile([P, S], U32, name="x_first", align_bytes=64)
+        nc.vector.tensor_copy(x_first[:], x_tab[0][:].bitcast(U32).indirect(offs_t[:]))
+        x_last = [keep.tile([P, S // 2], U32, name="x_last%d" % half, align_bytes=64) for half in range(2)]
         for half in range(2):
-            nc.vector.tensor_copy(x_g[1][:, 256 * half : 256 * (half + 1)], x_tab[1][:].bitcast(U32).indirect(offs_t[:, 16 * half : 16 * (half + 1)]))
+            nc.vector.tensor_copy(x_last[half][:], x_tab[1][:].bitcast(U32).indirect(offs_t[:, 16 * half : 16 * (half + 1)]))
 
-        hq = [keep.tile([P, P], U32, name="hq%d" % i, align_bytes=64) for i in range(TILES)]
-        hs = [keep.tile([P, P], U8, name="hs%d" % i, align_bytes=64) for i in range(TILES)]
+        spare = psum.tile([P, S], F32, name="spare", tag="y2")
+        for t in range(WARM):
+            wc = slice(t * P, (t + 1) * P)
+            nc.tensor.matmul_mx(
+                out=spare[:],
+                lhsT=wq[1][:, wc].bitcast(FP8X4),
+                lhsT_scale=ws[1][:, wc],
+                rhs=wq[1][:].bitcast(FP8X4),
+                rhs_scale=ws[1][:],
+                start=True,
+                stop=True,
+            )
+
         h_bf = [keep.tile([P, P, 4], BF16, name="h_bf%d" % i, align_bytes=64) for i in range(TILES)]
-        for i in range(TILES):
-            cols = slice(i * P, (i + 1) * P)
-            acc = psum.tile([P, 4, P], F32, name="h%d" % i)
-            for t in range(4):
-                wc = slice(t * P, (t + 1) * P)
-                for o in range(PASSES):
-                    nc.tensor.matmul_mx(
-                        out=acc[:, t, :],
-                        lhsT=wq[:, o, wc].bitcast(FP8X4),
-                        lhsT_scale=ws[:, o, wc],
-                        rhs=x_g[o][:, cols].bitcast(FP8X4),
-                        rhs_scale=xs_g[4 * o : P, cols],
-                        start=(o == 0),
-                        stop=(o == PASSES - 1),
-                    )
-            nc.scalar.copy(h_bf[i][:], acc[:].rearrange("p t n -> p n t"))
+        acc = [psum.tile([P, 4, P], F32, name="h%d" % i) for i in range(TILES)]
 
-        def quant_h(i):
-            nc.vector.quantize_mx(out=hq[i][:].bitcast(FP8X4), scales=hs[i][:], in_=h_bf[i][:].rearrange("p n t -> p (n t)"))
+        def project(i, t, o):
+            cols = slice(i * P, (i + 1) * P)
+            wc = slice(t * P, (t + 1) * P)
+            words = x_first[:, cols] if o == 0 else x_last[i // 2][:, (i % 2) * P : (i % 2 + 1) * P]
+            nc.tensor.matmul_mx(
+                out=acc[i][:, t, :],
+                lhsT=wq[o][:, wc].bitcast(FP8X4),
+                lhsT_scale=ws[o][:, wc],
+                rhs=words.bitcast(FP8X4),
+                rhs_scale=xs_g[4 * o : P, cols],
+                start=(o == 0),
+                stop=(o == PASSES - 1),
+            )
+
+        for i in range(TILES):
+            project(i, 0, 0)
+        for i in range(TILES):
+            project(i, 0, 1)
+            for t in range(1, 4):
+                for o in range(PASSES):
+                    project(i, t, o)
+            nc.scalar.copy(h_bf[i][:], acc[i][:].rearrange("p t n -> p n t"))
 
         e_g = keep.tile([P, V], U32, name="e_g", align_bytes=64)
-        quant_h(0)
         nc.vector.tensor_copy(e_g[:], e_tab[:].bitcast(U32).indirect(pro_t[:]))
-        for i in range(1, TILES):
-            quant_h(i)
 
-        for i in range(TILES):
+        ys = {}
+        pairs = {}
+
+        def product(i):
+            if i % 2 == 0:
+                pairs[i // 2] = keep.tile([P, 2 * P], U32, name="hq%d" % i, tag="e_tab", align_bytes=64)
+            hq = pairs[i // 2][:, (i % 2) * P : (i % 2 + 1) * P]
+            hs = keep.tile([P, P], U8, name="hs%d" % i, align_bytes=64)
+            nc.vector.quantize_mx(out=hq.bitcast(FP8X4), scales=hs[:], in_=h_bf[i][:].rearrange("p n t -> p (n t)"))
             y = psum.tile([P, V], F32, name="y%d" % i, tag="y%d" % i)
             nc.tensor.matmul_mx(
                 out=y[:],
-                lhsT=hq[i][:].bitcast(FP8X4),
-                lhsT_scale=hs[i][:],
+                lhsT=hq.bitcast(FP8X4),
+                lhsT_scale=hs[:],
                 rhs=e_g[:].bitcast(FP8X4),
                 rhs_scale=es_g[E_ROW:P, :],
                 start=True,
                 stop=True,
             )
-            z = keep.tile([P, V], F32, name="z%d" % i)
+            ys[i] = y
+
+        product(0)
+        product(1)
+        for i in range(TILES):
+            z = keep.tile([P, V], F32, name="z%d" % i, tag="z%d" % (i % 2))
             neg_max = keep.tile([P, 1], F32, name="neg_max%d" % i)
             total = keep.tile([P, 1], F32, name="total%d" % i)
             recip = keep.tile([P, 1], F32, name="recip%d" % i)
             ex = keep.tile([P, V], F32, name="ex%d" % i)
             res = keep.tile([P, V], F32, name="res%d" % i)
-            nc.vector.tensor_tensor(z[:], y[:], inv_b[:], ALU.mult)
+            nc.vector.tensor_tensor(z[:], ys[i][:], inv_b[:], ALU.mult)
+            if i + 2 < TILES:
+                product(i + 2)
             nc.vector.tensor_reduce(neg_max[:], z[:], AX.X, ALU.max, negate=True)
             nc.scalar.activation(ex[:], z[:], ACT.Exp, bias=neg_max[:], accum_out=total[:])
             nc.vector.reciprocal(recip[:], total[:])
             if i < TILES - 1:
-                nc.scalar.activation(res[:], ex[:], ACT.Copy, scale=recip[:])
+                nc.gpsimd.tensor_scalar(res[:], ex[:], recip[:], 0.0, ALU.mult, ALU.add)
             else:
                 nc.vector.tensor_scalar(res[:], ex[:], recip[:], None, ALU.mult)
             nc.sync.dma_start(out[i * P : (i + 1) * P, :], res[:])

@@ -20,6 +20,7 @@ PASSES = K // 512
 TILES = S // P
 E_ROW = 8
 WARM = 3
+SPLIT = 320
 
 FLOPS = 2 * K * H * S + 2 * H * S * V
 
@@ -32,10 +33,9 @@ def tile_picked_yphi_soft_p_kernel(tc, x_words, x_scales, w1, e_words, e_scales,
 
         offs_t = keep.tile([P, S // 16], U16, name="offs_t")
         pro_t = keep.tile([P, V // 16], U16, name="pro_t")
-        w_raw = [keep.tile([P, 4, H], F32, name="w_raw%d" % o, tag="w_raw%d" % o) for o in range(PASSES)]
-        x_tab = [keep.tile([P, T], I32, name="x_tab%d" % o) for o in range(PASSES)]
-        e_tab = keep.tile([P, W], I32, name="e_tab", tag="e_tab", align_bytes=64)
-        xs_tab = keep.tile([P, T], U8, name="xs_tab")
+        w_raw = [keep.tile([P, 4, H], F32, name="w_raw%d" % o, tag="w_raw%d" % o, align_bytes=64) for o in range(PASSES)]
+        x_tab = {0: keep.tile([P, T], I32, name="x_tab0")}
+        xs_tab = keep.tile([P, T], U8, name="xs_tab", tag="xs_tab")
         es_tab = keep.tile([P, W], U8, name="es_tab", tag="es_tab", align_bytes=64)
         inv_tab = keep.tile([P, W], F32, name="inv_tab")
         ident = keep.tile([P, P], F32, name="ident")
@@ -54,64 +54,65 @@ def tile_picked_yphi_soft_p_kernel(tc, x_words, x_scales, w1, e_words, e_scales,
         def load_x(o):
             nc.sync.dma_start(x_tab[o][:], x_words[o].rearrange("p n t -> p (n t)").bitcast(I32))
 
-        def load_xs(n):
-            o, q = divmod(n, 4)
-            nc.sync.dma_start(xs_tab[32 * q + 4 * o : 32 * q + 4 * o + 4, :].bitcast(I32), x_scales[o, 4 * q : 4 * q + 4, :].bitcast(I32))
-
-        def load_es(q):
-            nc.sync.dma_start(es_tab[32 * q + E_ROW : 32 * q + E_ROW + 4, :].bitcast(I32), e_scales[0, 4 * q : 4 * q + 4, :].bitcast(I32))
-
         nc.scalar.dma_start(inv_tab[P - 1 : P, :], inv[0:1, :])
         nc.sync.dma_start(pro_t[:], pro)
         nc.sync.dma_start(offs_t[:], offs)
         load_w(0)
-        for n in range(6):
-            load_xs(n)
+        nc.sync.dma_start(xs_tab[32:96:2, :].bitcast(I32), x_scales.rearrange("o q c -> q o c").bitcast(I32))
+        nc.sync.dma_start(es_tab[32:96:4, :].bitcast(I32), e_scales[0].bitcast(I32))
         load_w(1)
-        for n in range(6, 8):
-            load_xs(n)
-        for q in range(4):
-            load_es(q)
         load_x(0)
-        load_x(1)
-        nc.sync.dma_start(e_tab[:], e_words[0].rearrange("p n t -> p (n t)").bitcast(I32))
+
+        def place(plane, gathered):
+            for r in range(4):
+                nc.sync.dma_start(plane[r:P:4, :].bitcast(I32), gathered[32 + 4 * r : 96 + 4 * r : 2, :].bitcast(I32))
 
         wq = {}
         ws = [keep.tile([P, H], U8, name="ws%d" % o, align_bytes=64) for o in range(PASSES)]
         w_bf = [keep.tile([P, 4 * H], BF16, name="w_bf%d" % o, align_bytes=64) for o in range(PASSES)]
 
-        def cast_w(o):
-            nc.scalar.copy(
-                w_bf[o][:].rearrange("p (t m j) -> p m j t", t=4, j=4),
-                w_raw[o][:].rearrange("p j (m t) -> p m j t", t=4),
+        def cast_w(o, copy, ms):
+            copy(
+                w_bf[o][:].rearrange("p (t m j) -> p m j t", t=4, j=4)[:, ms],
+                w_raw[o][:].rearrange("p j (m t) -> p m j t", t=4)[:, ms],
             )
 
         def quant_w(o):
-            wq[o] = keep.tile([P, H], U32, name="wq%d" % o, tag=("wq0", "es_tab")[o], align_bytes=64)
+            wq[o] = keep.tile([P, H], U32, name="wq%d" % o, align_bytes=64)
             nc.vector.quantize_mx(out=wq[o][:].bitcast(FP8X4), scales=ws[o][:], in_=w_bf[o][:])
-
-        cast_w(0)
-        cast_w(1)
 
         inv_g = keep.tile([P, V], F32, name="inv_g")
         nc.vector.tensor_copy(inv_g[:], inv_tab[:].indirect(pro_t[:]))
+        xs_g = keep.tile([P, S], U8, name="xs_g")
+        nc.vector.tensor_copy(xs_g[:], xs_tab[:].indirect(offs_t[:]))
+        xs_p = keep.tile([P, S], U8, name="xs_p", align_bytes=64)
+        place(xs_p, xs_g)
+        x_tab[1] = keep.tile([P, T], I32, name="x_tab1", tag="xs_tab")
+        load_x(1)
+        es_g = keep.tile([P, V], U8, name="es_g")
+        nc.vector.tensor_copy(es_g[:], es_tab[:].indirect(pro_t[:]))
+        e_tab = keep.tile([P, W], I32, name="e_tab", tag="es_tab", align_bytes=64)
+        nc.sync.dma_start(e_tab[:], e_words[0].rearrange("p n t -> p (n t)").bitcast(I32))
+        es_p = keep.tile([P, V], U8, name="es_p", align_bytes=64)
+        place(es_p, es_g)
+
+        cast_w(0, nc.scalar.copy, slice(0, P))
+        quant_w(0)
+        cast_w(1, nc.scalar.copy, slice(0, P // 2))
+        cast_w(1, nc.vector.tensor_copy, slice(P // 2, P))
+        quant_w(1)
+
         turned = psum.tile([P, 4, P], F32, name="turned", tag="y0")
         for b in range(4):
             nc.tensor.transpose(turned[:, b, :], inv_g[:, b * P : (b + 1) * P], ident[:])
-        inv_col = keep.tile([P, 4], F32, name="inv_col", tag="w_raw1")
+        inv_col = keep.tile([P, 4], F32, name="inv_col", tag="w_raw1", align_bytes=64)
         nc.scalar.copy(inv_col[:], turned[:, :, P - 1])
-        quant_w(0)
         spread = psum.tile([P, V], F32, name="spread", tag="y1")
         for b in range(4):
             nc.tensor.transpose(spread[:, b * P : (b + 1) * P], inv_col[:, b : b + 1].to_broadcast([P, P]), ident[:])
         inv_b = keep.tile([P, V], F32, name="inv_b")
         nc.scalar.copy(inv_b[:], spread[:])
 
-        xs_g = keep.tile([P, S], U8, name="xs_g", align_bytes=64)
-        nc.vector.tensor_copy(xs_g[:], xs_tab[:].indirect(offs_t[:]))
-        es_g = keep.tile([P, V], U8, name="es_g", align_bytes=64)
-        nc.vector.tensor_copy(es_g[:], es_tab[:].indirect(pro_t[:]))
-        quant_w(1)
         x_first = keep.tile([P, S], U32, name="x_first", align_bytes=64)
         nc.vector.tensor_copy(x_first[:], x_tab[0][:].bitcast(U32).indirect(offs_t[:]))
         x_last = [keep.tile([P, S // 2], U32, name="x_last%d" % half, align_bytes=64) for half in range(2)]
@@ -143,7 +144,7 @@ def tile_picked_yphi_soft_p_kernel(tc, x_words, x_scales, w1, e_words, e_scales,
                 lhsT=wq[o][:, wc].bitcast(FP8X4),
                 lhsT_scale=ws[o][:, wc],
                 rhs=words.bitcast(FP8X4),
-                rhs_scale=xs_g[4 * o : P, cols],
+                rhs_scale=xs_p[4 * o : P, cols],
                 start=(o == 0),
                 stop=(o == PASSES - 1),
             )
@@ -165,7 +166,7 @@ def tile_picked_yphi_soft_p_kernel(tc, x_words, x_scales, w1, e_words, e_scales,
 
         def product(i):
             if i % 2 == 0:
-                pairs[i // 2] = keep.tile([P, 2 * P], U32, name="hq%d" % i, tag="e_tab", align_bytes=64)
+                pairs[i // 2] = keep.tile([P, 2 * P], U32, name="hq%d" % i, tag="es_tab", align_bytes=64)
             hq = pairs[i // 2][:, (i % 2) * P : (i % 2 + 1) * P]
             hs = keep.tile([P, P], U8, name="hs%d" % i, align_bytes=64)
             nc.vector.quantize_mx(out=hq.bitcast(FP8X4), scales=hs[:], in_=h_bf[i][:].rearrange("p n t -> p (n t)"))
@@ -175,29 +176,48 @@ def tile_picked_yphi_soft_p_kernel(tc, x_words, x_scales, w1, e_words, e_scales,
                 lhsT=hq.bitcast(FP8X4),
                 lhsT_scale=hs[:],
                 rhs=e_g[:].bitcast(FP8X4),
-                rhs_scale=es_g[E_ROW:P, :],
+                rhs_scale=es_p[:],
                 start=True,
                 stop=True,
             )
             ys[i] = y
 
+        zs, recip, ex = {}, {}, {}
+
+        def scores(i, tag):
+            zs[i] = keep.tile([P, V], F32, name="z%d" % i, tag=tag)
+            nc.vector.tensor_tensor(zs[i][:], ys[i][:], inv_b[:], ALU.mult)
+
+        def exps(i):
+            neg_max = keep.tile([P, 1], F32, name="neg_max%d" % i)
+            total = keep.tile([P, 1], F32, name="total%d" % i)
+            recip[i] = keep.tile([P, 1], F32, name="recip%d" % i)
+            ex[i] = keep.tile([P, V], F32, name="ex%d" % i)
+            nc.vector.tensor_reduce(neg_max[:], zs[i][:], AX.X, ALU.max, negate=True)
+            nc.scalar.activation(ex[i][:], zs[i][:], ACT.Exp, bias=neg_max[:], accum_out=total[:])
+            nc.vector.reciprocal(recip[i][:], total[:])
+
+        def finish(i, engine):
+            res = keep.tile([P, V], F32, name="res%d" % i)
+            engine.tensor_scalar(res[:], ex[i][:], recip[i][:], 0.0, ALU.mult, ALU.add)
+            nc.sync.dma_start(out[i * P : (i + 1) * P, :], res[:])
+
+        def finish_split(i):
+            left = keep.tile([P, SPLIT], F32, name="left")
+            right = keep.tile([P, V - SPLIT], F32, name="right")
+            nc.vector.tensor_scalar(left[:], ex[i][:, :SPLIT], recip[i][:], None, ALU.mult)
+            nc.scalar.activation(right[:], ex[i][:, SPLIT:], ACT.Copy, scale=recip[i][:])
+            nc.sync.dma_start(out[i * P : (i + 1) * P, :SPLIT], left[:])
+            nc.scalar.dma_start(out[i * P : (i + 1) * P, SPLIT:], right[:])
+
         product(0)
         product(1)
         for i in range(TILES):
-            z = keep.tile([P, V], F32, name="z%d" % i, tag="z%d" % (i % 2))
-            neg_max = keep.tile([P, 1], F32, name="neg_max%d" % i)
-            total = keep.tile([P, 1], F32, name="total%d" % i)
-            recip = keep.tile([P, 1], F32, name="recip%d" % i)
-            ex = keep.tile([P, V], F32, name="ex%d" % i)
-            res = keep.tile([P, V], F32, name="res%d" % i)
-            nc.vector.tensor_tensor(z[:], ys[i][:], inv_b[:], ALU.mult)
+            scores(i, "z%d" % (i % 2))
             if i + 2 < TILES:
                 product(i + 2)
-            nc.vector.tensor_reduce(neg_max[:], z[:], AX.X, ALU.max, negate=True)
-            nc.scalar.activation(ex[:], z[:], ACT.Exp, bias=neg_max[:], accum_out=total[:])
-            nc.vector.reciprocal(recip[:], total[:])
+            exps(i)
             if i < TILES - 1:
-                nc.gpsimd.tensor_scalar(res[:], ex[:], recip[:], 0.0, ALU.mult, ALU.add)
+                finish(i, nc.gpsimd)
             else:
-                nc.vector.tensor_scalar(res[:], ex[:], recip[:], None, ALU.mult)
-            nc.sync.dma_start(out[i * P : (i + 1) * P, :], res[:])
+                finish_split(i)

@@ -44,8 +44,7 @@ def tile_picked_yphi_soft_p_kernel(tc, x_words, x_scales, w1, e_words, e_scales,
         nc.gpsimd.memset(xs_tab[:].bitcast(I32), 0)
         nc.vector.memset(es_tab[:].bitcast(I32), 0)
         nc.vector.memset(warm[:], 0.0)
-        nc.scalar.activation(warm[:, 1:2], warm[:, 0:1], ACT.Exp)
-        nc.vector.memset(inv_tab[0 : P - 1, :], 0.0)
+        nc.vector.memset(inv_tab[0 : P - 1, :].bitcast(I32), 0)
         make_identity(nc, ident[:])
 
         def load_w(o):
@@ -54,11 +53,12 @@ def tile_picked_yphi_soft_p_kernel(tc, x_words, x_scales, w1, e_words, e_scales,
         def load_x(o):
             nc.sync.dma_start(x_tab[o][:], x_words[o].rearrange("p n t -> p (n t)").bitcast(I32))
 
+        nc.scalar.dma_start(xs_tab[32:96:2, :].bitcast(I32), x_scales.rearrange("o q c -> q o c").bitcast(I32))
         nc.scalar.dma_start(inv_tab[P - 1 : P, :], inv[0:1, :])
-        nc.sync.dma_start(pro_t[:], pro)
+        nc.scalar.activation(warm[:, 1:2], warm[:, 0:1], ACT.Exp)
         nc.sync.dma_start(offs_t[:], offs)
+        nc.sync.dma_start(pro_t[:], pro)
         load_w(0)
-        nc.sync.dma_start(xs_tab[32:96:2, :].bitcast(I32), x_scales.rearrange("o q c -> q o c").bitcast(I32))
         nc.sync.dma_start(es_tab[32:96:4, :].bitcast(I32), e_scales[0].bitcast(I32))
         load_w(1)
         load_x(0)
@@ -81,21 +81,21 @@ def tile_picked_yphi_soft_p_kernel(tc, x_words, x_scales, w1, e_words, e_scales,
             wq[o] = keep.tile([P, H], U32, name="wq%d" % o, align_bytes=64)
             nc.vector.quantize_mx(out=wq[o][:].bitcast(FP8X4), scales=ws[o][:], in_=w_bf[o][:])
 
-        inv_g = keep.tile([P, V], F32, name="inv_g")
-        nc.vector.tensor_copy(inv_g[:], inv_tab[:].indirect(pro_t[:]))
         xs_g = keep.tile([P, S], U8, name="xs_g")
         nc.vector.tensor_copy(xs_g[:], xs_tab[:].indirect(offs_t[:]))
         xs_p = keep.tile([P, S], U8, name="xs_p", align_bytes=64)
         place(xs_p, xs_g)
         x_tab[1] = keep.tile([P, T], I32, name="x_tab1", tag="xs_tab")
         load_x(1)
-        es_g = keep.tile([P, V], U8, name="es_g")
+        es_g = keep.tile([P, V], U8, name="es_g", tag="es_g", align_bytes=64)
         nc.vector.tensor_copy(es_g[:], es_tab[:].indirect(pro_t[:]))
         e_tab = keep.tile([P, W], I32, name="e_tab", tag="es_tab", align_bytes=64)
         nc.sync.dma_start(e_tab[:], e_words[0].rearrange("p n t -> p (n t)").bitcast(I32))
         es_p = keep.tile([P, V], U8, name="es_p", align_bytes=64)
         place(es_p, es_g)
 
+        inv_g = keep.tile([P, V], F32, name="inv_g")
+        nc.vector.tensor_copy(inv_g[:], inv_tab[:].indirect(pro_t[:]))
         cast_w(0, nc.scalar.copy, slice(0, P))
         quant_w(0)
         cast_w(1, nc.scalar.copy, slice(0, P // 2))
@@ -132,8 +132,8 @@ def tile_picked_yphi_soft_p_kernel(tc, x_words, x_scales, w1, e_words, e_scales,
                 stop=True,
             )
 
-        h_bf = [keep.tile([P, P, 4], BF16, name="h_bf%d" % i, align_bytes=64) for i in range(TILES)]
-        acc = [psum.tile([P, 4, P], F32, name="h%d" % i) for i in range(TILES)]
+        h_bf = [keep.tile([P, P, 4], BF16, name="h_bf%d" % i, tag="h_bf%d" % i, align_bytes=64) for i in range(TILES)]
+        acc = [psum.tile([P, 4, P], F32, name="h%d" % i, tag="h%d" % i) for i in range(TILES)]
 
         def project(i, t, o):
             cols = slice(i * P, (i + 1) * P)
@@ -158,66 +158,80 @@ def tile_picked_yphi_soft_p_kernel(tc, x_words, x_scales, w1, e_words, e_scales,
                     project(i, t, o)
             nc.scalar.copy(h_bf[i][:], acc[i][:].rearrange("p t n -> p n t"))
 
-        e_g = keep.tile([P, V], U32, name="e_g", align_bytes=64)
-        nc.vector.tensor_copy(e_g[:], e_tab[:].bitcast(U32).indirect(pro_t[:]))
+        hq, hs, e_g = {}, {}, {}
+        halves = [slice(0, V // 2), slice(V // 2, V)]
 
-        ys = {}
-        pairs = {}
+        def gather_e(half):
+            e_g[half] = keep.tile([P, V // 2], U32, name="e_g%d" % half, tag=("e_g0", "h_bf0")[half], align_bytes=64)
+            nc.vector.tensor_copy(e_g[half][:], e_tab[:].bitcast(U32).indirect(pro_t[:, 16 * half : 16 * (half + 1)]))
 
-        def product(i):
-            if i % 2 == 0:
-                pairs[i // 2] = keep.tile([P, 2 * P], U32, name="hq%d" % i, tag="es_tab", align_bytes=64)
-            hq = pairs[i // 2][:, (i % 2) * P : (i % 2 + 1) * P]
-            hs = keep.tile([P, P], U8, name="hs%d" % i, align_bytes=64)
-            nc.vector.quantize_mx(out=hq.bitcast(FP8X4), scales=hs[:], in_=h_bf[i][:].rearrange("p n t -> p (n t)"))
-            y = psum.tile([P, V], F32, name="y%d" % i, tag="y%d" % i)
+        def quant_h(i):
+            hq[i] = keep.tile([P, P], U32, name="hq%d" % i, tag=("es_g", "es_tab")[i % 2], align_bytes=64)
+            hs[i] = keep.tile([P, P], U8, name="hs%d" % i, align_bytes=64)
+            nc.vector.quantize_mx(out=hq[i][:].bitcast(FP8X4), scales=hs[i][:], in_=h_bf[i][:].rearrange("p n t -> p (n t)"))
+
+        def product(i, half, dst):
             nc.tensor.matmul_mx(
-                out=y[:],
-                lhsT=hq.bitcast(FP8X4),
-                lhsT_scale=hs[:],
-                rhs=e_g[:].bitcast(FP8X4),
-                rhs_scale=es_p[:],
+                out=dst,
+                lhsT=hq[i][:].bitcast(FP8X4),
+                lhsT_scale=hs[i][:],
+                rhs=e_g[half][:].bitcast(FP8X4),
+                rhs_scale=es_p[:, halves[half]],
                 start=True,
                 stop=True,
             )
-            ys[i] = y
 
-        zs, recip, ex = {}, {}, {}
+        ys = {}
 
-        def scores(i, tag):
-            zs[i] = keep.tile([P, V], F32, name="z%d" % i, tag=tag)
-            nc.vector.tensor_tensor(zs[i][:], ys[i][:], inv_b[:], ALU.mult)
+        def products(i):
+            quant_h(i)
+            ys[i] = psum.tile([P, V], F32, name="y%d" % i, tag="y%d" % i)
+            for half in range(2):
+                product(i, half, ys[i][:, halves[half]])
+
+        gather_e(0)
+        quant_h(0)
+        gather_e(1)
+        y_first = [psum.tile([P, V // 2], F32, name="y0_%d" % half, tag=("y0", "h0")[half]) for half in range(2)]
+        for half in range(2):
+            product(0, half, y_first[half][:])
+        products(1)
+
+        zs, total, ex = {}, {}, {}
+
+        def scores(i):
+            zs[i] = keep.tile([P, V], F32, name="z%d" % i, tag="z%d" % (i % 2))
+            if i == 0:
+                for half in range(2):
+                    nc.vector.tensor_tensor(zs[0][:, halves[half]], y_first[half][:], inv_b[:, halves[half]], ALU.mult)
+            else:
+                nc.vector.tensor_tensor(zs[i][:], ys[i][:], inv_b[:], ALU.mult)
 
         def exps(i):
             neg_max = keep.tile([P, 1], F32, name="neg_max%d" % i)
-            total = keep.tile([P, 1], F32, name="total%d" % i)
-            recip[i] = keep.tile([P, 1], F32, name="recip%d" % i)
+            total[i] = keep.tile([P, 1], F32, name="total%d" % i)
             ex[i] = keep.tile([P, V], F32, name="ex%d" % i)
             nc.vector.tensor_reduce(neg_max[:], zs[i][:], AX.X, ALU.max, negate=True)
-            nc.scalar.activation(ex[i][:], zs[i][:], ACT.Exp, bias=neg_max[:], accum_out=total[:])
-            nc.vector.reciprocal(recip[i][:], total[:])
+            nc.scalar.activation(ex[i][:], zs[i][:], ACT.Exp, bias=neg_max[:], accum_out=total[i][:])
 
-        def finish(i, engine):
-            res = keep.tile([P, V], F32, name="res%d" % i)
-            engine.tensor_scalar(res[:], ex[i][:], recip[i][:], 0.0, ALU.mult, ALU.add)
-            nc.sync.dma_start(out[i * P : (i + 1) * P, :], res[:])
+        def finish(i, parts):
+            recip = keep.tile([P, 1], F32, name="recip%d" % i)
+            nc.vector.reciprocal(recip[:], total[i][:])
+            for cols, on_vector, queue in parts:
+                res = keep.tile([P, cols.stop - cols.start], F32, name="res%d_%d" % (i, cols.start))
+                if on_vector:
+                    nc.vector.tensor_scalar(res[:], ex[i][:, cols], recip[:], None, ALU.mult)
+                else:
+                    nc.scalar.activation(res[:], ex[i][:, cols], ACT.Copy, scale=recip[:])
+                queue.dma_start(out[i * P : (i + 1) * P, cols], res[:])
 
-        def finish_split(i):
-            left = keep.tile([P, SPLIT], F32, name="left")
-            right = keep.tile([P, V - SPLIT], F32, name="right")
-            nc.vector.tensor_scalar(left[:], ex[i][:, :SPLIT], recip[i][:], None, ALU.mult)
-            nc.scalar.activation(right[:], ex[i][:, SPLIT:], ACT.Copy, scale=recip[i][:])
-            nc.sync.dma_start(out[i * P : (i + 1) * P, :SPLIT], left[:])
-            nc.scalar.dma_start(out[i * P : (i + 1) * P, SPLIT:], right[:])
-
-        product(0)
-        product(1)
+        whole = slice(0, V)
         for i in range(TILES):
-            scores(i, "z%d" % (i % 2))
+            scores(i)
             if i + 2 < TILES:
-                product(i + 2)
+                products(i + 2)
+            if i in (1, 2):
+                finish(i - 1, [(whole, False, nc.sync)])
             exps(i)
-            if i < TILES - 1:
-                finish(i, nc.gpsimd)
-            else:
-                finish_split(i)
+        finish(2, [(whole, True, nc.sync)])
+        finish(3, [(slice(0, SPLIT), True, nc.sync), (slice(SPLIT, V), False, nc.scalar)])

@@ -15,11 +15,14 @@ ACT = mybir.ActivationFunctionType
 AX = mybir.AxisListType
 
 P = 128
-K, T, S, H, V, W = 1024, 2048, 512, 512, 512, 2048
-PASSES = K // 512
+K, T, S = 1024, 2048, 512
+H, W, V = 512, 2048, 512
+PACK = 4
+K_PASS = P * PACK
+PASSES = K // K_PASS
 TILES = S // P
-E_ROW = 8
-WARM = 3
+HALF = 256
+HALF_COLS = HALF // 16
 SPLIT = 320
 
 FLOPS = 2 * K * H * S + 2 * H * S * V
@@ -33,7 +36,7 @@ def tile_picked_yphi_soft_p_kernel(tc, x_words, x_scales, w1, e_words, e_scales,
 
         offs_t = keep.tile([P, S // 16], U16, name="offs_t")
         pro_t = keep.tile([P, V // 16], U16, name="pro_t")
-        w_raw = [keep.tile([P, 4, H], F32, name="w_raw%d" % o, tag="w_raw%d" % o, align_bytes=64) for o in range(PASSES)]
+        w_raw = [keep.tile([P, PACK, H], F32, name="w_raw%d" % o, tag="w_raw%d" % o, align_bytes=64) for o in range(PASSES)]
         x_tab = {0: keep.tile([P, T], I32, name="x_tab0")}
         xs_tab = keep.tile([P, T], U8, name="xs_tab", tag="xs_tab")
         es_tab = keep.tile([P, W], U8, name="es_tab", tag="es_tab", align_bytes=64)
@@ -44,16 +47,17 @@ def tile_picked_yphi_soft_p_kernel(tc, x_words, x_scales, w1, e_words, e_scales,
         nc.gpsimd.memset(xs_tab[:].bitcast(I32), 0)
         nc.vector.memset(es_tab[:].bitcast(I32), 0)
         nc.vector.memset(warm[:], 0.0)
-        nc.vector.memset(inv_tab[0 : P - 1, :].bitcast(I32), 0)
+        nc.vector.memset(inv_tab[0 : P - 1, :], 0.0)
         make_identity(nc, ident[:])
 
         def load_w(o):
-            nc.sync.dma_start(w_raw[o][:], w1[512 * o : 512 * (o + 1), :].rearrange("(p j) c -> p j c", j=4))
+            rows = w1[K_PASS * o : K_PASS * (o + 1), :]
+            nc.sync.dma_start(w_raw[o][:], rows.rearrange("(p j) c -> p j c", j=PACK))
 
         def load_x(o):
             nc.sync.dma_start(x_tab[o][:], x_words[o].rearrange("p n t -> p (n t)").bitcast(I32))
 
-        nc.scalar.dma_start(xs_tab[32:96:2, :].bitcast(I32), x_scales.rearrange("o q c -> q o c").bitcast(I32))
+        nc.scalar.dma_start(xs_tab[32:96:2, :].bitcast(I32), x_scales.rearrange("o g c -> g o c").bitcast(I32))
         nc.scalar.dma_start(inv_tab[P - 1 : P, :], inv[0:1, :])
         nc.scalar.activation(warm[:, 1:2], warm[:, 0:1], ACT.Exp)
         nc.sync.dma_start(offs_t[:], offs)
@@ -69,12 +73,12 @@ def tile_picked_yphi_soft_p_kernel(tc, x_words, x_scales, w1, e_words, e_scales,
 
         wq = {}
         ws = [keep.tile([P, H], U8, name="ws%d" % o, align_bytes=64) for o in range(PASSES)]
-        w_bf = [keep.tile([P, 4 * H], BF16, name="w_bf%d" % o, align_bytes=64) for o in range(PASSES)]
+        w_bf = [keep.tile([P, PACK * H], BF16, name="w_bf%d" % o, align_bytes=64) for o in range(PASSES)]
 
         def cast_w(o, copy, ms):
             copy(
-                w_bf[o][:].rearrange("p (t m j) -> p m j t", t=4, j=4)[:, ms],
-                w_raw[o][:].rearrange("p j (m t) -> p m j t", t=4)[:, ms],
+                w_bf[o][:].rearrange("p (t m j) -> p m j t", t=PACK, j=PACK)[:, ms],
+                w_raw[o][:].rearrange("p j (m t) -> p m j t", t=PACK)[:, ms],
             )
 
         def quant_w(o):
@@ -102,38 +106,29 @@ def tile_picked_yphi_soft_p_kernel(tc, x_words, x_scales, w1, e_words, e_scales,
         cast_w(1, nc.vector.tensor_copy, slice(P // 2, P))
         quant_w(1)
 
-        turned = psum.tile([P, 4, P], F32, name="turned", tag="y0")
-        for b in range(4):
-            nc.tensor.transpose(turned[:, b, :], inv_g[:, b * P : (b + 1) * P], ident[:])
-        inv_col = keep.tile([P, 4], F32, name="inv_col", tag="w_raw1", align_bytes=64)
-        nc.scalar.copy(inv_col[:], turned[:, :, P - 1])
+        inv_t = psum.tile([P, V // P, P], F32, name="inv_t", tag="y0")
+        for b in range(V // P):
+            nc.tensor.transpose(inv_t[:, b, :], inv_g[:, b * P : (b + 1) * P], ident[:])
+        inv_col = keep.tile([P, V // P], F32, name="inv_col", tag="w_raw1", align_bytes=64)
+        nc.scalar.copy(inv_col[:], inv_t[:, :, P - 1])
         spread = psum.tile([P, V], F32, name="spread", tag="y1")
-        for b in range(4):
+        for b in range(V // P):
             nc.tensor.transpose(spread[:, b * P : (b + 1) * P], inv_col[:, b : b + 1].to_broadcast([P, P]), ident[:])
         inv_b = keep.tile([P, V], F32, name="inv_b")
         nc.scalar.copy(inv_b[:], spread[:])
 
         x_first = keep.tile([P, S], U32, name="x_first", align_bytes=64)
         nc.vector.tensor_copy(x_first[:], x_tab[0][:].bitcast(U32).indirect(offs_t[:]))
-        x_last = [keep.tile([P, S // 2], U32, name="x_last%d" % half, align_bytes=64) for half in range(2)]
+        x_last = [keep.tile([P, HALF], U32, name="x_last%d" % half, align_bytes=64) for half in range(2)]
         for half in range(2):
-            nc.vector.tensor_copy(x_last[half][:], x_tab[1][:].bitcast(U32).indirect(offs_t[:, 16 * half : 16 * (half + 1)]))
+            entries = offs_t[:, HALF_COLS * half : HALF_COLS * (half + 1)]
+            nc.vector.tensor_copy(x_last[half][:], x_tab[1][:].bitcast(U32).indirect(entries))
 
-        spare = psum.tile([P, S], F32, name="spare", tag="y2")
-        for t in range(WARM):
-            wc = slice(t * P, (t + 1) * P)
-            nc.tensor.matmul_mx(
-                out=spare[:],
-                lhsT=wq[1][:, wc].bitcast(FP8X4),
-                lhsT_scale=ws[1][:, wc],
-                rhs=wq[1][:].bitcast(FP8X4),
-                rhs_scale=ws[1][:],
-                start=True,
-                stop=True,
-            )
-
-        h_bf = [keep.tile([P, P, 4], BF16, name="h_bf%d" % i, tag="h_bf%d" % i, align_bytes=64) for i in range(TILES)]
-        acc = [psum.tile([P, 4, P], F32, name="h%d" % i, tag="h%d" % i) for i in range(TILES)]
+        h_bf = {
+            first: keep.tile([P, count * P, PACK], BF16, name="h_bf%d" % first, tag="h_bf%d" % first, align_bytes=64)
+            for first, count in ((0, 1), (1, 2), (3, 1))
+        }
+        acc = [psum.tile([P, PACK, P], F32, name="h%d" % i, tag="h%d" % i) for i in range(TILES)]
 
         def project(i, t, o):
             cols = slice(i * P, (i + 1) * P)
@@ -153,59 +148,75 @@ def tile_picked_yphi_soft_p_kernel(tc, x_words, x_scales, w1, e_words, e_scales,
             project(i, 0, 0)
         for i in range(TILES):
             project(i, 0, 1)
-            for t in range(1, 4):
+            for t in range(1, PACK):
                 for o in range(PASSES):
                     project(i, t, o)
-            nc.scalar.copy(h_bf[i][:], acc[i][:].rearrange("p t n -> p n t"))
+            first = 1 if i == 2 else i
+            nc.scalar.copy(h_bf[first][:, (i - first) * P : (i - first + 1) * P, :], acc[i][:].rearrange("p t n -> p n t"))
 
         hq, hs, e_g = {}, {}, {}
-        halves = [slice(0, V // 2), slice(V // 2, V)]
+        halves = [slice(0, HALF), slice(HALF, V)]
 
-        def gather_e(half):
-            e_g[half] = keep.tile([P, V // 2], U32, name="e_g%d" % half, tag=("e_g0", "h_bf0")[half], align_bytes=64)
-            nc.vector.tensor_copy(e_g[half][:], e_tab[:].bitcast(U32).indirect(pro_t[:, 16 * half : 16 * (half + 1)]))
+        def gather_e(half, tag):
+            e_g[half] = keep.tile([P, HALF], U32, name="e_g%d" % half, tag=tag, align_bytes=64)
+            entries = pro_t[:, HALF_COLS * half : HALF_COLS * (half + 1)]
+            nc.vector.tensor_copy(e_g[half][:], e_tab[:].bitcast(U32).indirect(entries))
 
-        def quant_h(i):
-            hq[i] = keep.tile([P, P], U32, name="hq%d" % i, tag=("es_g", "es_tab")[i % 2], align_bytes=64)
-            hs[i] = keep.tile([P, P], U8, name="hs%d" % i, align_bytes=64)
-            nc.vector.quantize_mx(out=hq[i][:].bitcast(FP8X4), scales=hs[i][:], in_=h_bf[i][:].rearrange("p n t -> p (n t)"))
+        def quant_h(first, count, tag):
+            codes = keep.tile([P, count * P], U32, name="hq%d" % first, tag=tag, align_bytes=64)
+            scales = keep.tile([P, count * P], U8, name="hs%d" % first, align_bytes=64)
+            nc.vector.quantize_mx(out=codes[:].bitcast(FP8X4), scales=scales[:], in_=h_bf[first][:].rearrange("p n t -> p (n t)"))
+            hq[first] = codes[:].bitcast(FP8X4)
+            hs[first] = scales[:]
 
         def product(i, half, dst):
             nc.tensor.matmul_mx(
                 out=dst,
-                lhsT=hq[i][:].bitcast(FP8X4),
-                lhsT_scale=hs[i][:],
+                lhsT=hq[i],
+                lhsT_scale=hs[i],
                 rhs=e_g[half][:].bitcast(FP8X4),
                 rhs_scale=es_p[:, halves[half]],
                 start=True,
                 stop=True,
             )
 
-        ys = {}
-
-        def products(i):
-            quant_h(i)
-            ys[i] = psum.tile([P, V], F32, name="y%d" % i, tag="y%d" % i)
-            for half in range(2):
-                product(i, half, ys[i][:, halves[half]])
-
-        gather_e(0)
-        quant_h(0)
-        gather_e(1)
-        y_first = [psum.tile([P, V // 2], F32, name="y0_%d" % half, tag=("y0", "h0")[half]) for half in range(2)]
-        for half in range(2):
-            product(0, half, y_first[half][:])
-        products(1)
-
         zs, total, ex = {}, {}, {}
 
-        def scores(i):
-            zs[i] = keep.tile([P, V], F32, name="z%d" % i, tag="z%d" % (i % 2))
-            if i == 0:
-                for half in range(2):
-                    nc.vector.tensor_tensor(zs[0][:, halves[half]], y_first[half][:], inv_b[:, halves[half]], ALU.mult)
-            else:
-                nc.vector.tensor_tensor(zs[i][:], ys[i][:], inv_b[:], ALU.mult)
+        gather_e(0, "e_g0")
+        quant_h(0, 1, "es_g")
+        gather_e(1, "h_bf0")
+        y_first = [psum.tile([P, HALF], F32, name="y0_%d" % half, tag=("y0", "h0")[half]) for half in range(2)]
+        for half in range(2):
+            product(0, half, y_first[half][:])
+
+        quant_h(1, 2, "es_tab")
+        y_turned = [psum.tile([P, 2, 2 * P], F32, name="y_turned%d" % half, tag="y%d" % (half + 1)) for half in range(2)]
+        z_turned = [keep.tile([P, 2 * P], F32, name="z_turned%d" % b) for b in range(V // P)]
+        for b in range(V // P):
+            nc.tensor.matmul_mx(
+                out=y_turned[b // 2][:, b % 2, :],
+                lhsT=e_g[b // 2][:, (b % 2) * P : (b % 2 + 1) * P].bitcast(FP8X4),
+                lhsT_scale=es_p[:, b * P : (b + 1) * P],
+                rhs=hq[1],
+                rhs_scale=hs[1],
+                start=True,
+                stop=True,
+            )
+        for b in range(V // P):
+            nc.scalar.activation(z_turned[b][:], y_turned[b // 2][:, b % 2, :], ACT.Copy, scale=inv_col[:, b : b + 1])
+
+        zs[0] = keep.tile([P, V], F32, name="z0")
+        for half in range(2):
+            nc.vector.tensor_tensor(zs[0][:, halves[half]], y_first[half][:], inv_b[:, halves[half]], ALU.mult)
+
+        quant_h(3, 1, "es_g")
+        y_last = psum.tile([P, V], F32, name="y3", tag="y3")
+        for half in range(2):
+            product(3, half, y_last[:, halves[half]])
+        for i in (1, 2):
+            zs[i] = psum.tile([P, V], F32, name="z%d" % i, tag="h%d" % i)
+            for b in range(V // P):
+                nc.tensor.transpose(zs[i][:, b * P : (b + 1) * P], z_turned[b][:, (i - 1) * P : i * P], ident[:])
 
         def exps(i):
             neg_max = keep.tile([P, 1], F32, name="neg_max%d" % i)
@@ -214,24 +225,25 @@ def tile_picked_yphi_soft_p_kernel(tc, x_words, x_scales, w1, e_words, e_scales,
             nc.vector.tensor_reduce(neg_max[:], zs[i][:], AX.X, ALU.max, negate=True)
             nc.scalar.activation(ex[i][:], zs[i][:], ACT.Exp, bias=neg_max[:], accum_out=total[i][:])
 
-        def finish(i, parts):
+        def finish(i, vector_cols):
+            samples = slice(i * P, (i + 1) * P)
             recip = keep.tile([P, 1], F32, name="recip%d" % i)
             nc.vector.reciprocal(recip[:], total[i][:])
-            for cols, on_vector, queue in parts:
-                res = keep.tile([P, cols.stop - cols.start], F32, name="res%d_%d" % (i, cols.start))
-                if on_vector:
-                    nc.vector.tensor_scalar(res[:], ex[i][:, cols], recip[:], None, ALU.mult)
-                else:
-                    nc.scalar.activation(res[:], ex[i][:, cols], ACT.Copy, scale=recip[:])
-                queue.dma_start(out[i * P : (i + 1) * P, cols], res[:])
+            left = keep.tile([P, vector_cols], F32, name="left%d" % i)
+            nc.vector.tensor_scalar(left[:], ex[i][:, :vector_cols], recip[:], None, ALU.mult)
+            nc.sync.dma_start(out[samples, :vector_cols], left[:])
+            if vector_cols < V:
+                right = keep.tile([P, V - vector_cols], F32, name="right%d" % i)
+                nc.scalar.activation(right[:], ex[i][:, vector_cols:], ACT.Copy, scale=recip[:])
+                nc.scalar.dma_start(out[samples, vector_cols:], right[:])
 
-        whole = slice(0, V)
-        for i in range(TILES):
-            scores(i)
-            if i + 2 < TILES:
-                products(i + 2)
-            if i in (1, 2):
-                finish(i - 1, [(whole, False, nc.sync)])
-            exps(i)
-        finish(2, [(whole, True, nc.sync)])
-        finish(3, [(slice(0, SPLIT), True, nc.sync), (slice(SPLIT, V), False, nc.scalar)])
+        exps(0)
+        zs[3] = keep.tile([P, V], F32, name="z3")
+        nc.vector.tensor_tensor(zs[3][:], y_last[:], inv_b[:], ALU.mult)
+        exps(3)
+        finish(0, V)
+        exps(1)
+        exps(2)
+        finish(3, V)
+        finish(1, V)
+        finish(2, SPLIT)

@@ -24,6 +24,7 @@ TILES = S // P
 HALF = 256
 HALF_COLS = HALF // 16
 SPLIT = 320
+LATE_BYTES = 4096
 
 FLOPS = 2 * K * H * S + 2 * H * S * V
 
@@ -32,6 +33,8 @@ def tile_picked_yphi_soft_p_kernel(tc, x_words, x_scales, w1, e_words, e_scales,
     nc = tc.nc
     with ExitStack() as ctx:
         keep = ctx.enter_context(tc.tile_pool(name="keep", bufs=1))
+        late = ctx.enter_context(tc.tile_pool(name="late", bufs=1))
+        stats = ctx.enter_context(tc.tile_pool(name="stats", bufs=1))
         psum = ctx.enter_context(tc.psum_pool(name="psum", bufs=1))
 
         offs_t = keep.tile([P, S // 16], U16, name="offs_t")
@@ -88,15 +91,15 @@ def tile_picked_yphi_soft_p_kernel(tc, x_words, x_scales, w1, e_words, e_scales,
         xs_g = keep.tile([P, S], U8, name="xs_g")
         nc.vector.tensor_copy(xs_g[:], xs_tab[:].indirect(offs_t[:]))
         xs_p = keep.tile([P, S], U8, name="xs_p", align_bytes=64)
-        place(xs_p, xs_g)
+        place(xs_p, xs_g[:])
         x_tab[1] = keep.tile([P, T], I32, name="x_tab1", tag="xs_tab")
         load_x(1)
-        es_g = keep.tile([P, V], U8, name="es_g", tag="es_g", align_bytes=64)
-        nc.vector.tensor_copy(es_g[:], es_tab[:].indirect(pro_t[:]))
+        es_g = late.tile([P, LATE_BYTES], U8, name="es_g", align_bytes=64, offset=0)
+        nc.vector.tensor_copy(es_g[:, :V], es_tab[:].indirect(pro_t[:]))
         e_tab = keep.tile([P, W], I32, name="e_tab", tag="es_tab", align_bytes=64)
         nc.sync.dma_start(e_tab[:], e_words[0].rearrange("p n t -> p (n t)").bitcast(I32))
         es_p = keep.tile([P, V], U8, name="es_p", align_bytes=64)
-        place(es_p, es_g)
+        place(es_p, es_g[:, :V])
 
         inv_g = keep.tile([P, V], F32, name="inv_g")
         nc.vector.tensor_copy(inv_g[:], inv_tab[:].indirect(pro_t[:]))
@@ -124,10 +127,7 @@ def tile_picked_yphi_soft_p_kernel(tc, x_words, x_scales, w1, e_words, e_scales,
             entries = offs_t[:, HALF_COLS * half : HALF_COLS * (half + 1)]
             nc.vector.tensor_copy(x_last[half][:], x_tab[1][:].bitcast(U32).indirect(entries))
 
-        h_bf = {
-            first: keep.tile([P, count * P, PACK], BF16, name="h_bf%d" % first, tag="h_bf%d" % first, align_bytes=64)
-            for first, count in ((0, 1), (1, 2), (3, 1))
-        }
+        h_bf = [keep.tile([P, P, PACK], BF16, name="h_bf%d" % i, align_bytes=64) for i in range(TILES)]
         acc = [psum.tile([P, PACK, P], F32, name="h%d" % i, tag="h%d" % i) for i in range(TILES)]
 
         def project(i, t, o):
@@ -144,106 +144,138 @@ def tile_picked_yphi_soft_p_kernel(tc, x_words, x_scales, w1, e_words, e_scales,
                 stop=(o == PASSES - 1),
             )
 
+        idle = psum.tile([P, S], F32, name="idle", tag="y3")
+
+        def warm_up(words, scales):
+            nc.tensor.matmul_mx(
+                out=idle[:],
+                lhsT=wq[1][:, :P].bitcast(FP8X4),
+                lhsT_scale=ws[1][:, :P],
+                rhs=words.bitcast(FP8X4),
+                rhs_scale=scales,
+                start=True,
+                stop=True,
+            )
+
+        for repeat in range(2):
+            warm_up(wq[0][:], ws[0][:])
         for i in range(TILES):
             project(i, 0, 0)
+        warm_up(x_first[:], xs_p[:])
         for i in range(TILES):
             project(i, 0, 1)
             for t in range(1, PACK):
                 for o in range(PASSES):
                     project(i, t, o)
-            first = 1 if i == 2 else i
-            nc.scalar.copy(h_bf[first][:, (i - first) * P : (i - first + 1) * P, :], acc[i][:].rearrange("p t n -> p n t"))
+            nc.scalar.copy(h_bf[i][:], acc[i][:].rearrange("p t n -> p n t"))
 
         hq, hs, e_g = {}, {}, {}
         halves = [slice(0, HALF), slice(HALF, V)]
+        e_g[0] = keep.tile([P, HALF], U32, name="e_g0", align_bytes=64)
+        e_g[1] = late.tile([P, HALF], U32, name="e_g1", align_bytes=64, offset=4 * S + S)
+        for i in range(TILES):
+            hq[i] = late.tile([P, P], U32, name="hq%d" % i, align_bytes=64, offset=4 * P * (1 if i == 3 else i))
+            hs[i] = late.tile([P, P], U8, name="hs%d" % i, align_bytes=64, offset=4 * S + P * i)
 
-        def gather_e(half, tag):
-            e_g[half] = keep.tile([P, HALF], U32, name="e_g%d" % half, tag=tag, align_bytes=64)
+        def gather_e(half):
             entries = pro_t[:, HALF_COLS * half : HALF_COLS * (half + 1)]
             nc.vector.tensor_copy(e_g[half][:], e_tab[:].bitcast(U32).indirect(entries))
 
-        def quant_h(first, count, tag):
-            codes = keep.tile([P, count * P], U32, name="hq%d" % first, tag=tag, align_bytes=64)
-            scales = keep.tile([P, count * P], U8, name="hs%d" % first, align_bytes=64)
-            nc.vector.quantize_mx(out=codes[:].bitcast(FP8X4), scales=scales[:], in_=h_bf[first][:].rearrange("p n t -> p (n t)"))
-            hq[first] = codes[:].bitcast(FP8X4)
-            hs[first] = scales[:]
+        def quant_h(i):
+            nc.vector.quantize_mx(out=hq[i][:].bitcast(FP8X4), scales=hs[i][:], in_=h_bf[i][:].rearrange("p n t -> p (n t)"))
 
         def product(i, half, dst):
             nc.tensor.matmul_mx(
                 out=dst,
-                lhsT=hq[i],
-                lhsT_scale=hs[i],
+                lhsT=hq[i][:].bitcast(FP8X4),
+                lhsT_scale=hs[i][:],
                 rhs=e_g[half][:].bitcast(FP8X4),
                 rhs_scale=es_p[:, halves[half]],
                 start=True,
                 stop=True,
             )
 
-        zs, total, ex = {}, {}, {}
+        blocks = V // P
+        ys = {i: psum.tile([P, V], F32, name="y%d" % i, tag="y%d" % i) for i in range(TILES)}
+        z_turned = {(i, b): keep.tile([P, P], F32, name="z_turned%d_%d" % (i, b)) for i in (1, 2) for b in range(blocks)}
+        zs, total, ex, recip = {}, {}, {}, {}
 
-        gather_e(0, "e_g0")
-        quant_h(0, 1, "es_g")
-        gather_e(1, "h_bf0")
-        y_first = [psum.tile([P, HALF], F32, name="y0_%d" % half, tag=("y0", "h0")[half]) for half in range(2)]
-        for half in range(2):
-            product(0, half, y_first[half][:])
-
-        quant_h(1, 2, "es_tab")
-        y_turned = [psum.tile([P, 2, 2 * P], F32, name="y_turned%d" % half, tag="y%d" % (half + 1)) for half in range(2)]
-        z_turned = [keep.tile([P, 2 * P], F32, name="z_turned%d" % b) for b in range(V // P)]
-        for b in range(V // P):
+        def turned(b, first, dst):
             nc.tensor.matmul_mx(
-                out=y_turned[b // 2][:, b % 2, :],
+                out=dst,
                 lhsT=e_g[b // 2][:, (b % 2) * P : (b % 2 + 1) * P].bitcast(FP8X4),
                 lhsT_scale=es_p[:, b * P : (b + 1) * P],
-                rhs=hq[1],
-                rhs_scale=hs[1],
+                rhs=hq[first][:].bitcast(FP8X4),
+                rhs_scale=hs[first][:],
                 start=True,
                 stop=True,
             )
-        for b in range(V // P):
-            nc.scalar.activation(z_turned[b][:], y_turned[b // 2][:, b % 2, :], ACT.Copy, scale=inv_col[:, b : b + 1])
 
-        zs[0] = keep.tile([P, V], F32, name="z0")
-        for half in range(2):
-            nc.vector.tensor_tensor(zs[0][:, halves[half]], y_first[half][:], inv_b[:, halves[half]], ALU.mult)
+        def scale_turned(b, dst, src):
+            nc.scalar.activation(dst, src, ACT.Copy, scale=inv_col[:, b : b + 1])
 
-        quant_h(3, 1, "es_g")
-        y_last = psum.tile([P, V], F32, name="y3", tag="y3")
+        def turn_back(i, b, src):
+            nc.tensor.transpose(zs[i][:, b * P : (b + 1) * P], src, ident[:])
+
+        def plain(i):
+            zs[i] = keep.tile([P, V], F32, name="z%d" % i)
+            nc.vector.tensor_tensor(zs[i][:], ys[i][:], inv_b[:], ALU.mult)
+
+        gather_e(0)
+        quant_h(0)
+        gather_e(1)
         for half in range(2):
-            product(3, half, y_last[:, halves[half]])
+            product(0, half, ys[0][:, halves[half]])
+        for i in (1, 2):
+            quant_h(i)
+            for b in range(blocks):
+                turned(b, i, ys[i][:, b * P : (b + 1) * P])
+        plain(0)
+        quant_h(3)
+        for half in range(2):
+            product(3, half, ys[3][:, halves[half]])
         for i in (1, 2):
             zs[i] = psum.tile([P, V], F32, name="z%d" % i, tag="h%d" % i)
-            for b in range(V // P):
-                nc.tensor.transpose(zs[i][:, b * P : (b + 1) * P], z_turned[b][:, (i - 1) * P : i * P], ident[:])
+            for b in range(blocks):
+                scale_turned(b, z_turned[i, b][:], ys[i][:, b * P : (b + 1) * P])
+            for b in range(blocks):
+                turn_back(i, b, z_turned[i, b][:])
 
         def exps(i):
-            neg_max = keep.tile([P, 1], F32, name="neg_max%d" % i)
+            width, place_at = {0: (16, 0), 1: (8, 64), 2: (8, 0), 3: (8, 32)}[i]
+            neg_max = stats.tile([P, width], F32, name="neg_max%d" % i, offset=place_at)[:, 0:1]
             total[i] = keep.tile([P, 1], F32, name="total%d" % i)
             ex[i] = keep.tile([P, V], F32, name="ex%d" % i)
-            nc.vector.tensor_reduce(neg_max[:], zs[i][:], AX.X, ALU.max, negate=True)
-            nc.scalar.activation(ex[i][:], zs[i][:], ACT.Exp, bias=neg_max[:], accum_out=total[i][:])
+            nc.vector.tensor_reduce(neg_max, zs[i][:], AX.X, ALU.max, negate=True)
+            nc.scalar.activation(ex[i][:], zs[i][:], ACT.Exp, bias=neg_max, accum_out=total[i][:])
 
-        def finish(i, vector_cols):
-            samples = slice(i * P, (i + 1) * P)
-            recip = keep.tile([P, 1], F32, name="recip%d" % i)
-            nc.vector.reciprocal(recip[:], total[i][:])
-            left = keep.tile([P, vector_cols], F32, name="left%d" % i)
-            nc.vector.tensor_scalar(left[:], ex[i][:, :vector_cols], recip[:], None, ALU.mult)
-            nc.sync.dma_start(out[samples, :vector_cols], left[:])
-            if vector_cols < V:
-                right = keep.tile([P, V - vector_cols], F32, name="right%d" % i)
-                nc.scalar.activation(right[:], ex[i][:, vector_cols:], ACT.Copy, scale=recip[:])
-                nc.scalar.dma_start(out[samples, vector_cols:], right[:])
+        def invert(i):
+            recip[i] = keep.tile([P, 1], F32, name="recip%d" % i)
+            nc.vector.reciprocal(recip[i][:], total[i][:])
 
+        def finish(i, cols, engine):
+            part = keep.tile([P, cols.stop - cols.start], F32, name="part%d_%d" % (i, cols.start))
+            if engine == "vector":
+                nc.vector.tensor_scalar(part[:], ex[i][:, cols], recip[i][:], None, ALU.mult)
+            elif engine == "gpsimd":
+                nc.gpsimd.tensor_scalar(part[:], ex[i][:, cols], recip[i][:], 1.0, ALU.mult, ALU.mult)
+            else:
+                nc.scalar.activation(part[:], ex[i][:, cols], ACT.Copy, scale=recip[i][:])
+            queue = nc.scalar if engine == "scalar" else nc.sync
+            queue.dma_start(out[i * P : (i + 1) * P, cols], part[:])
+
+        whole = slice(0, V)
         exps(0)
-        zs[3] = keep.tile([P, V], F32, name="z3")
-        nc.vector.tensor_tensor(zs[3][:], y_last[:], inv_b[:], ALU.mult)
-        exps(3)
-        finish(0, V)
+        plain(3)
         exps(1)
+        invert(0)
+        finish(0, whole, "gpsimd")
+        exps(3)
         exps(2)
-        finish(3, V)
-        finish(1, V)
-        finish(2, SPLIT)
+        invert(1)
+        invert(3)
+        finish(1, whole, "vector")
+        finish(3, whole, "vector")
+        invert(2)
+        finish(2, slice(0, SPLIT), "vector")
+        finish(2, slice(SPLIT, V), "scalar")

@@ -91,9 +91,9 @@ def tile_picked_yphi_soft_p_kernel(tc, x_words, x_scales, w1, e_words, e_scales,
         xs_g = keep.tile([P, S], U8, name="xs_g")
         nc.vector.tensor_copy(xs_g[:], xs_tab[:].indirect(offs_t[:]))
         xs_p = keep.tile([P, S], U8, name="xs_p", align_bytes=64)
-        place(xs_p, xs_g[:])
         x_tab[1] = keep.tile([P, T], I32, name="x_tab1", tag="xs_tab")
         load_x(1)
+        place(xs_p, xs_g[:])
         es_g = late.tile([P, LATE_BYTES], U8, name="es_g", align_bytes=64, offset=0)
         nc.vector.tensor_copy(es_g[:, :V], es_tab[:].indirect(pro_t[:]))
         e_tab = keep.tile([P, W], I32, name="e_tab", tag="es_tab", align_bytes=64)
@@ -159,9 +159,9 @@ def tile_picked_yphi_soft_p_kernel(tc, x_words, x_scales, w1, e_words, e_scales,
 
         for repeat in range(2):
             warm_up(wq[0][:], ws[0][:])
+        warm_up(x_first[:], ws[0][:])
         for i in range(TILES):
             project(i, 0, 0)
-        warm_up(x_first[:], xs_p[:])
         for i in range(TILES):
             project(i, 0, 1)
             for t in range(1, PACK):
@@ -196,7 +196,8 @@ def tile_picked_yphi_soft_p_kernel(tc, x_words, x_scales, w1, e_words, e_scales,
             )
 
         blocks = V // P
-        ys = {i: psum.tile([P, V], F32, name="y%d" % i, tag="y%d" % i) for i in range(TILES)}
+        ys = {i: psum.tile([P, V], F32, name="y%d" % i, tag="y%d" % i) for i in range(1, TILES)}
+        y_first = [psum.tile([P, HALF], F32, name="y0_%d" % half, tag=("y0", "h0")[half]) for half in range(2)]
         z_turned = {(i, b): keep.tile([P, P], F32, name="z_turned%d_%d" % (i, b)) for i in (1, 2) for b in range(blocks)}
         zs, total, ex, recip = {}, {}, {}, {}
 
@@ -225,13 +226,15 @@ def tile_picked_yphi_soft_p_kernel(tc, x_words, x_scales, w1, e_words, e_scales,
         quant_h(0)
         gather_e(1)
         for half in range(2):
-            product(0, half, ys[0][:, halves[half]])
+            product(0, half, y_first[half][:])
         for i in (1, 2):
             quant_h(i)
             for b in range(blocks):
                 turned(b, i, ys[i][:, b * P : (b + 1) * P])
-        plain(0)
+        zs[0] = keep.tile([P, V], F32, name="z0")
+        nc.vector.tensor_tensor(zs[0][:, halves[0]], y_first[0][:], inv_b[:, halves[0]], ALU.mult)
         quant_h(3)
+        nc.vector.tensor_tensor(zs[0][:, halves[1]], y_first[1][:], inv_b[:, halves[1]], ALU.mult)
         for half in range(2):
             product(3, half, ys[3][:, halves[half]])
         for i in (1, 2):

@@ -196,9 +196,10 @@ def tile_picked_yphi_soft_p_kernel(tc, x_words, x_scales, w1, e_words, e_scales,
             )
 
         blocks = V // P
-        ys = {i: psum.tile([P, V], F32, name="y%d" % i, tag="y%d" % i) for i in range(1, TILES)}
+        ys = {i: psum.tile([P, V], F32, name="y%d" % i, tag="y%d" % i) for i in (1, 3)}
+        y_shared = [psum.tile([P, HALF], F32, name="y2_%d" % half, tag=("y2", "h2")[half]) for half in range(2)]
         y_first = [psum.tile([P, HALF], F32, name="y0_%d" % half, tag=("y0", "h0")[half]) for half in range(2)]
-        z_turned = {(i, b): keep.tile([P, P], F32, name="z_turned%d_%d" % (i, b)) for i in (1, 2) for b in range(blocks)}
+        z_turned = {(i, b): keep.tile([P, P], F32, name="z_turned%d_%d" % (i, b)) for i in (1, 2, 3) for b in range(blocks)}
         zs, total, ex, recip = {}, {}, {}, {}
 
         def turned(b, first, dst):
@@ -227,25 +228,33 @@ def tile_picked_yphi_soft_p_kernel(tc, x_words, x_scales, w1, e_words, e_scales,
         gather_e(1)
         for half in range(2):
             product(0, half, y_first[half][:])
+        def scores(i, b):
+            if i == 2:
+                return y_shared[b // 2][:, (b % 2) * P : (b % 2 + 1) * P]
+            return ys[i][:, b * P : (b + 1) * P]
+
         for i in (1, 2):
             quant_h(i)
             for b in range(blocks):
-                turned(b, i, ys[i][:, b * P : (b + 1) * P])
+                turned(b, i, scores(i, b))
         zs[0] = keep.tile([P, V], F32, name="z0")
         nc.vector.tensor_tensor(zs[0][:, halves[0]], y_first[0][:], inv_b[:, halves[0]], ALU.mult)
         quant_h(3)
         nc.vector.tensor_tensor(zs[0][:, halves[1]], y_first[1][:], inv_b[:, halves[1]], ALU.mult)
-        for half in range(2):
-            product(3, half, ys[3][:, halves[half]])
-        for i in (1, 2):
-            zs[i] = psum.tile([P, V], F32, name="z%d" % i, tag="h%d" % i)
+        for b in range(blocks):
+            turned(b, 3, scores(3, b))
+        for i in (1, 2, 3):
+            zs[i] = psum.tile([P, V], F32, name="z%d" % i, tag={1: "h1", 2: "h3", 3: "y0"}[i])
             for b in range(blocks):
-                scale_turned(b, z_turned[i, b][:], ys[i][:, b * P : (b + 1) * P])
+                if i == 2 and b < 2:
+                    nc.vector.tensor_scalar(z_turned[i, b][:], scores(i, b), inv_col[:, b : b + 1], None, ALU.mult)
+                else:
+                    scale_turned(b, z_turned[i, b][:], scores(i, b))
             for b in range(blocks):
                 turn_back(i, b, z_turned[i, b][:])
 
         def exps(i):
-            width, place_at = {0: (16, 0), 1: (8, 64), 2: (8, 0), 3: (8, 32)}[i]
+            width, place_at = {0: (8, 0), 1: (8, 32), 2: (8, 64), 3: (8, 0)}[i]
             neg_max = stats.tile([P, width], F32, name="neg_max%d" % i, offset=place_at)[:, 0:1]
             total[i] = keep.tile([P, 1], F32, name="total%d" % i)
             ex[i] = keep.tile([P, V], F32, name="ex%d" % i)
@@ -269,16 +278,16 @@ def tile_picked_yphi_soft_p_kernel(tc, x_words, x_scales, w1, e_words, e_scales,
 
         whole = slice(0, V)
         exps(0)
-        plain(3)
         exps(1)
-        invert(0)
-        finish(0, whole, "gpsimd")
-        exps(3)
         exps(2)
+        invert(0)
+        finish(0, halves[1], "gpsimd")
+        exps(3)
         invert(1)
-        invert(3)
+        finish(0, halves[0], "vector")
         finish(1, whole, "vector")
-        finish(3, whole, "vector")
         invert(2)
-        finish(2, slice(0, SPLIT), "vector")
-        finish(2, slice(SPLIT, V), "scalar")
+        finish(2, whole, "vector")
+        invert(3)
+        finish(3, slice(0, SPLIT), "vector")
+        finish(3, slice(SPLIT, V), "scalar")

@@ -174,7 +174,7 @@ def tile_picked_yphi_soft_p_kernel(tc, x_words, x_scales, w1, e_words, e_scales,
         e_g[0] = keep.tile([P, HALF], U32, name="e_g0", align_bytes=64)
         e_g[1] = late.tile([P, HALF], U32, name="e_g1", align_bytes=64, offset=4 * S + S)
         for i in range(TILES):
-            hq[i] = late.tile([P, P], U32, name="hq%d" % i, align_bytes=64, offset=4 * P * (1 if i == 3 else i))
+            hq[i] = late.tile([P, P], U32, name="hq%d" % i, align_bytes=64, offset=4 * P * (i % 3))
             hs[i] = late.tile([P, P], U8, name="hs%d" % i, align_bytes=64, offset=4 * S + P * i)
 
         def gather_e(half):
@@ -199,7 +199,9 @@ def tile_picked_yphi_soft_p_kernel(tc, x_words, x_scales, w1, e_words, e_scales,
         ys = {i: psum.tile([P, V], F32, name="y%d" % i, tag="y%d" % i) for i in (1, 3)}
         y_shared = [psum.tile([P, HALF], F32, name="y2_%d" % half, tag=("y2", "h2")[half]) for half in range(2)]
         y_first = [psum.tile([P, HALF], F32, name="y0_%d" % half, tag=("y0", "h0")[half]) for half in range(2)]
-        z_turned = {(i, b): keep.tile([P, P], F32, name="z_turned%d_%d" % (i, b)) for i in (1, 2, 3) for b in range(blocks)}
+        pair = keep.tile([P, 2, P], F32, name="z_turned_pair")
+        z_turned = {(i, b): keep.tile([P, P], F32, name="z_turned%d_%d" % (i, b))[:] for i in (1, 2, 3) for b in range(blocks) if i != 2 or b > 1}
+        z_turned[2, 0], z_turned[2, 1] = pair[:, 0, :], pair[:, 1, :]
         zs, total, ex, recip = {}, {}, {}, {}
 
         def turned(b, first, dst):
@@ -243,23 +245,32 @@ def tile_picked_yphi_soft_p_kernel(tc, x_words, x_scales, w1, e_words, e_scales,
         nc.vector.tensor_tensor(zs[0][:, halves[1]], y_first[1][:], inv_b[:, halves[1]], ALU.mult)
         for b in range(blocks):
             turned(b, 3, scores(3, b))
-        for i in (1, 2, 3):
+        def turn(i):
             zs[i] = psum.tile([P, V], F32, name="z%d" % i, tag={1: "h1", 2: "h3", 3: "y0"}[i])
             for b in range(blocks):
-                if i == 2 and b < 2:
-                    nc.vector.tensor_scalar(z_turned[i, b][:], scores(i, b), inv_col[:, b : b + 1], None, ALU.mult)
-                else:
-                    scale_turned(b, z_turned[i, b][:], scores(i, b))
+                if (i, b) == (2, 0):
+                    factors = inv_col[:, 0:2].unsqueeze(2).to_broadcast([P, 2, P])
+                    nc.vector.tensor_tensor(pair[:], y_shared[0][:].rearrange("p (b n) -> p b n", b=2), factors, ALU.mult)
+                elif (i, b) != (2, 1):
+                    scale_turned(b, z_turned[i, b], scores(i, b))
             for b in range(blocks):
-                turn_back(i, b, z_turned[i, b][:])
+                turn_back(i, b, z_turned[i, b])
 
-        def exps(i):
+        neg_max = {}
+
+        def row_max(i):
             width, place_at = {0: (8, 0), 1: (8, 32), 2: (8, 64), 3: (8, 0)}[i]
-            neg_max = stats.tile([P, width], F32, name="neg_max%d" % i, offset=place_at)[:, 0:1]
+            neg_max[i] = stats.tile([P, width], F32, name="neg_max%d" % i, offset=place_at)[:, 0:1]
+            nc.vector.tensor_reduce(neg_max[i], zs[i][:], AX.X, ALU.max, negate=True)
+
+        def exp(i):
             total[i] = keep.tile([P, 1], F32, name="total%d" % i)
             ex[i] = keep.tile([P, V], F32, name="ex%d" % i)
-            nc.vector.tensor_reduce(neg_max, zs[i][:], AX.X, ALU.max, negate=True)
-            nc.scalar.activation(ex[i][:], zs[i][:], ACT.Exp, bias=neg_max, accum_out=total[i][:])
+            nc.scalar.activation(ex[i][:], zs[i][:], ACT.Exp, bias=neg_max[i], accum_out=total[i][:])
+
+        def exps(i):
+            row_max(i)
+            exp(i)
 
         def invert(i):
             recip[i] = keep.tile([P, 1], F32, name="recip%d" % i)
@@ -277,7 +288,11 @@ def tile_picked_yphi_soft_p_kernel(tc, x_words, x_scales, w1, e_words, e_scales,
             queue.dma_start(out[i * P : (i + 1) * P, cols], part[:])
 
         whole = slice(0, V)
-        exps(0)
+        turn(1)
+        turn(2)
+        row_max(0)
+        turn(3)
+        exp(0)
         exps(1)
         exps(2)
         invert(0)

@@ -24,6 +24,7 @@ TILES = S // P
 HALF = 256
 HALF_COLS = HALF // 16
 SPLIT = 320
+CAST = 40
 LATE_BYTES = 4096
 
 FLOPS = 2 * K * H * S + 2 * H * S * V
@@ -67,8 +68,8 @@ def tile_picked_yphi_soft_p_kernel(tc, x_words, x_scales, w1, e_words, e_scales,
         nc.sync.dma_start(pro_t[:], pro)
         load_w(0)
         nc.sync.dma_start(es_tab[32:96:4, :].bitcast(I32), e_scales[0].bitcast(I32))
-        load_w(1)
         load_x(0)
+        load_w(1)
 
         def place(plane, gathered):
             for r in range(4):
@@ -92,8 +93,12 @@ def tile_picked_yphi_soft_p_kernel(tc, x_words, x_scales, w1, e_words, e_scales,
         nc.vector.tensor_copy(xs_g[:], xs_tab[:].indirect(offs_t[:]))
         xs_p = keep.tile([P, S], U8, name="xs_p", align_bytes=64)
         x_tab[1] = keep.tile([P, T], I32, name="x_tab1", tag="xs_tab")
-        load_x(1)
         place(xs_p, xs_g[:])
+        load_x(1)
+        inv_g = keep.tile([P, V], F32, name="inv_g")
+        nc.vector.tensor_copy(inv_g[:], inv_tab[:].indirect(pro_t[:]))
+        cast_w(0, nc.scalar.copy, slice(0, CAST))
+        cast_w(0, nc.vector.tensor_copy, slice(CAST, P))
         es_g = late.tile([P, LATE_BYTES], U8, name="es_g", align_bytes=64, offset=0)
         nc.vector.tensor_copy(es_g[:, :V], es_tab[:].indirect(pro_t[:]))
         e_tab = keep.tile([P, W], I32, name="e_tab", tag="es_tab", align_bytes=64)
@@ -101,18 +106,14 @@ def tile_picked_yphi_soft_p_kernel(tc, x_words, x_scales, w1, e_words, e_scales,
         es_p = keep.tile([P, V], U8, name="es_p", align_bytes=64)
         place(es_p, es_g[:, :V])
 
-        inv_g = keep.tile([P, V], F32, name="inv_g")
-        nc.vector.tensor_copy(inv_g[:], inv_tab[:].indirect(pro_t[:]))
-        cast_w(0, nc.scalar.copy, slice(0, P))
         quant_w(0)
-        cast_w(1, nc.scalar.copy, slice(0, P // 2))
-        cast_w(1, nc.vector.tensor_copy, slice(P // 2, P))
-        quant_w(1)
+        x_first = keep.tile([P, S], U32, name="x_first", align_bytes=64)
+        nc.vector.tensor_copy(x_first[:], x_tab[0][:].bitcast(U32).indirect(offs_t[:]))
 
         inv_t = psum.tile([P, V // P, P], F32, name="inv_t", tag="y0")
         for b in range(V // P):
             nc.tensor.transpose(inv_t[:, b, :], inv_g[:, b * P : (b + 1) * P], ident[:])
-        inv_col = keep.tile([P, V // P], F32, name="inv_col", tag="w_raw1", align_bytes=64)
+        inv_col = keep.tile([P, V // P], F32, name="inv_col", tag="w_raw0", align_bytes=64)
         nc.scalar.copy(inv_col[:], inv_t[:, :, P - 1])
         spread = psum.tile([P, V], F32, name="spread", tag="y1")
         for b in range(V // P):
@@ -120,8 +121,9 @@ def tile_picked_yphi_soft_p_kernel(tc, x_words, x_scales, w1, e_words, e_scales,
         inv_b = keep.tile([P, V], F32, name="inv_b")
         nc.scalar.copy(inv_b[:], spread[:])
 
-        x_first = keep.tile([P, S], U32, name="x_first", align_bytes=64)
-        nc.vector.tensor_copy(x_first[:], x_tab[0][:].bitcast(U32).indirect(offs_t[:]))
+        cast_w(1, nc.scalar.copy, slice(0, CAST))
+        cast_w(1, nc.vector.tensor_copy, slice(CAST, P))
+        quant_w(1)
         x_last = [keep.tile([P, HALF], U32, name="x_last%d" % half, align_bytes=64) for half in range(2)]
         for half in range(2):
             entries = offs_t[:, HALF_COLS * half : HALF_COLS * (half + 1)]
@@ -140,34 +142,18 @@ def tile_picked_yphi_soft_p_kernel(tc, x_words, x_scales, w1, e_words, e_scales,
                 lhsT_scale=ws[o][:, wc],
                 rhs=words.bitcast(FP8X4),
                 rhs_scale=xs_p[4 * o : P, cols],
-                start=(o == 0),
-                stop=(o == PASSES - 1),
+                start=(o == 0 and t == 0),
+                stop=(o == PASSES - 1 and t == PACK - 1),
             )
 
-        idle = psum.tile([P, S], F32, name="idle", tag="y3")
-
-        def warm_up(words, scales):
-            nc.tensor.matmul_mx(
-                out=idle[:],
-                lhsT=wq[1][:, :P].bitcast(FP8X4),
-                lhsT_scale=ws[1][:, :P],
-                rhs=words.bitcast(FP8X4),
-                rhs_scale=scales,
-                start=True,
-                stop=True,
-            )
-
-        for repeat in range(2):
-            warm_up(wq[0][:], ws[0][:])
-        warm_up(x_first[:], ws[0][:])
         for i in range(TILES):
-            project(i, 0, 0)
+            for t in range(PACK):
+                project(i, t, 0)
         for i in range(TILES):
-            project(i, 0, 1)
-            for t in range(1, PACK):
-                for o in range(PASSES):
-                    project(i, t, o)
-            nc.scalar.copy(h_bf[i][:], acc[i][:].rearrange("p t n -> p n t"))
+            for t in range(PACK):
+                project(i, t, 1)
+            copy = nc.vector.tensor_copy if i == 0 else nc.scalar.copy
+            copy(h_bf[i][:], acc[i][:].rearrange("p t n -> p n t"))
 
         hq, hs, e_g = {}, {}, {}
         halves = [slice(0, HALF), slice(HALF, V)]

@@ -48,7 +48,8 @@ def tile_picked_yphi_soft_p_kernel(tc, x_words, x_scales, w1, e_words, e_scales,
         ident = keep.tile([P, P], F32, name="ident")
         warm = keep.tile([P, 8], F32, name="warm")
 
-        nc.gpsimd.memset(xs_tab[:].bitcast(I32), 0)
+        nc.gpsimd.memset(xs_tab[0:32, :].bitcast(I32), 0)
+        nc.vector.memset(xs_tab[64:P, :].bitcast(I32), 0)
         nc.vector.memset(es_tab[:].bitcast(I32), 0)
         nc.vector.memset(warm[:], 0.0)
         nc.vector.memset(inv_tab[0 : P - 1, :], 0.0)
@@ -61,19 +62,19 @@ def tile_picked_yphi_soft_p_kernel(tc, x_words, x_scales, w1, e_words, e_scales,
         def load_x(o):
             nc.sync.dma_start(x_tab[o][:], x_words[o].rearrange("p n t -> p (n t)").bitcast(I32))
 
-        nc.scalar.dma_start(xs_tab[32:96:2, :].bitcast(I32), x_scales.rearrange("o g c -> g o c").bitcast(I32))
+        nc.scalar.dma_start(xs_tab[32:64, :].bitcast(I32), x_scales.rearrange("o g c -> g o c").bitcast(I32))
         nc.scalar.dma_start(inv_tab[P - 1 : P, :], inv[0:1, :])
         nc.scalar.activation(warm[:, 1:2], warm[:, 0:1], ACT.Exp)
         nc.sync.dma_start(offs_t[:], offs)
-        nc.sync.dma_start(pro_t[:], pro)
         load_w(0)
+        nc.sync.dma_start(pro_t[:], pro)
         nc.sync.dma_start(es_tab[32:96:4, :].bitcast(I32), e_scales[0].bitcast(I32))
         load_x(0)
         load_w(1)
 
-        def place(plane, gathered):
+        def place(plane, gathered, step):
             for r in range(4):
-                nc.sync.dma_start(plane[r:P:4, :].bitcast(I32), gathered[32 + 4 * r : 96 + 4 * r : 2, :].bitcast(I32))
+                nc.sync.dma_start(plane[r:P:4, :].bitcast(I32), gathered[32 + 2 * step * r : 32 + 2 * step * r + 32 * step : step, :].bitcast(I32))
 
         wq = {}
         ws = [keep.tile([P, H], U8, name="ws%d" % o, align_bytes=64) for o in range(PASSES)]
@@ -93,22 +94,21 @@ def tile_picked_yphi_soft_p_kernel(tc, x_words, x_scales, w1, e_words, e_scales,
         nc.vector.tensor_copy(xs_g[:], xs_tab[:].indirect(offs_t[:]))
         xs_p = keep.tile([P, S], U8, name="xs_p", align_bytes=64)
         x_tab[1] = keep.tile([P, T], I32, name="x_tab1", tag="xs_tab")
-        place(xs_p, xs_g[:])
+        place(xs_p, xs_g[:], 1)
         load_x(1)
         inv_g = keep.tile([P, V], F32, name="inv_g")
         nc.vector.tensor_copy(inv_g[:], inv_tab[:].indirect(pro_t[:]))
-        cast_w(0, nc.scalar.copy, slice(0, CAST))
-        cast_w(0, nc.vector.tensor_copy, slice(CAST, P))
+        cast_w(0, nc.scalar.copy, slice(0, P))
         es_g = late.tile([P, LATE_BYTES], U8, name="es_g", align_bytes=64, offset=0)
         nc.vector.tensor_copy(es_g[:, :V], es_tab[:].indirect(pro_t[:]))
         e_tab = keep.tile([P, W], I32, name="e_tab", tag="es_tab", align_bytes=64)
         nc.sync.dma_start(e_tab[:], e_words[0].rearrange("p n t -> p (n t)").bitcast(I32))
         es_p = keep.tile([P, V], U8, name="es_p", align_bytes=64)
-        place(es_p, es_g[:, :V])
+        place(es_p, es_g[:, :V], 2)
 
-        quant_w(0)
         x_first = keep.tile([P, S], U32, name="x_first", align_bytes=64)
         nc.vector.tensor_copy(x_first[:], x_tab[0][:].bitcast(U32).indirect(offs_t[:]))
+        quant_w(0)
 
         inv_t = psum.tile([P, V // P, P], F32, name="inv_t", tag="y0")
         for b in range(V // P):

@@ -149,11 +149,25 @@ def tile_picked_yphi_soft_p_kernel(tc, x_words, x_scales, w1, e_words, e_scales,
         for i in range(TILES):
             for t in range(PACK):
                 project(i, t, 0)
+        idle = psum.tile([P, S], F32, name="idle", tag="y3")
+
+        def warm_up(words):
+            nc.tensor.matmul_mx(
+                out=idle[:],
+                lhsT=words[:, :P].bitcast(FP8X4),
+                lhsT_scale=ws[1][:, :P],
+                rhs=x_first[:].bitcast(FP8X4),
+                rhs_scale=xs_p[:],
+                start=True,
+                stop=True,
+            )
+
+        warm_up(wq[1])
         for i in range(TILES):
             for t in range(PACK):
                 project(i, t, 1)
-            copy = nc.vector.tensor_copy if i == 0 else nc.scalar.copy
-            copy(h_bf[i][:], acc[i][:].rearrange("p t n -> p n t"))
+            nc.scalar.copy(h_bf[i][:], acc[i][:].rearrange("p t n -> p n t"))
+        warm_up(x_last[1])
 
         hq, hs, e_g = {}, {}, {}
         halves = [slice(0, HALF), slice(HALF, V)]
@@ -212,6 +226,7 @@ def tile_picked_yphi_soft_p_kernel(tc, x_words, x_scales, w1, e_words, e_scales,
             nc.vector.tensor_tensor(zs[i][:], ys[i][:], inv_b[:], ALU.mult)
 
         gather_e(0)
+        warm_up(e_g[0])
         quant_h(0)
         gather_e(1)
         for half in range(2):

@@ -196,7 +196,8 @@ def tile_picked_yphi_soft_p_kernel(tc, x_words, x_scales, w1, e_words, e_scales,
             )
 
         blocks = V // P
-        ys = {i: psum.tile([P, V], F32, name="y%d" % i, tag="y%d" % i) for i in (1, 3)}
+        ys = {3: psum.tile([P, V], F32, name="y3", tag="y3")}
+        y_second = [psum.tile([P, HALF], F32, name="y1_%d" % half, tag=("y1", "h3")[half]) for half in range(2)]
         y_shared = [psum.tile([P, HALF], F32, name="y2_%d" % half, tag=("y2", "h2")[half]) for half in range(2)]
         y_first = [psum.tile([P, HALF], F32, name="y0_%d" % half, tag=("y0", "h0")[half]) for half in range(2)]
         pair = keep.tile([P, 2, P], F32, name="z_turned_pair")
@@ -227,19 +228,25 @@ def tile_picked_yphi_soft_p_kernel(tc, x_words, x_scales, w1, e_words, e_scales,
 
         gather_e(0)
         warm_up(e_g[0])
-        quant_h(0)
-        gather_e(1)
-        for half in range(2):
-            product(0, half, y_first[half][:])
         def scores(i, b):
             if i == 2:
                 return y_shared[b // 2][:, (b % 2) * P : (b % 2 + 1) * P]
+            if i == 1:
+                return y_second[b // 2][:, (b % 2) * P : (b % 2 + 1) * P]
             return ys[i][:, b * P : (b + 1) * P]
 
-        for i in (1, 2):
-            quant_h(i)
-            for b in range(blocks):
-                turned(b, i, scores(i, b))
+        quant_h(0)
+        quant_h(1)
+        gather_e(1)
+        for b in range(2):
+            turned(b, 1, scores(1, b))
+        for half in range(2):
+            product(0, half, y_first[half][:])
+        for b in range(2, blocks):
+            turned(b, 1, scores(1, b))
+        quant_h(2)
+        for b in range(blocks):
+            turned(b, 2, scores(2, b))
         zs[0] = keep.tile([P, V], F32, name="z0")
         nc.vector.tensor_tensor(zs[0][:, halves[0]], y_first[0][:], inv_b[:, halves[0]], ALU.mult)
         quant_h(3)

@@ -174,7 +174,7 @@ def tile_picked_yphi_soft_p_kernel(tc, x_words, x_scales, w1, e_words, e_scales,
         e_g[0] = keep.tile([P, HALF], U32, name="e_g0", align_bytes=64)
         e_g[1] = late.tile([P, HALF], U32, name="e_g1", align_bytes=64, offset=4 * S + S)
         for i in range(TILES):
-            hq[i] = late.tile([P, P], U32, name="hq%d" % i, align_bytes=64, offset=4 * P * (i % 3))
+            hq[i] = late.tile([P, P], U32, name="hq%d" % i, align_bytes=64, offset=4 * P * i)
             hs[i] = late.tile([P, P], U8, name="hs%d" % i, align_bytes=64, offset=4 * S + P * i)
 
         def gather_e(half):

@@ -129,7 +129,7 @@ def tile_picked_yphi_soft_p_kernel(tc, x_words, x_scales, w1, e_words, e_scales,
             entries = offs_t[:, HALF_COLS * half : HALF_COLS * (half + 1)]
             nc.vector.tensor_copy(x_last[half][:], x_tab[1][:].bitcast(U32).indirect(entries))
 
-        h_bf = [keep.tile([P, P, PACK], BF16, name="h_bf%d" % i, align_bytes=64) for i in range(TILES)]
+        h_bf = [keep.tile([P, 2, P, PACK], BF16, name="h_bf%d" % g, align_bytes=64) for g in range(2)]
         acc = [psum.tile([P, PACK, P], F32, name="h%d" % i, tag="h%d" % i) for i in range(TILES)]
 
         def project(i, t, o):
@@ -166,29 +166,32 @@ def tile_picked_yphi_soft_p_kernel(tc, x_words, x_scales, w1, e_words, e_scales,
         for i in range(TILES):
             for t in range(PACK):
                 project(i, t, 1)
-            nc.scalar.copy(h_bf[i][:], acc[i][:].rearrange("p t n -> p n t"))
+            copy = nc.vector.tensor_copy if i == 0 else nc.scalar.copy
+            copy(h_bf[i // 2][:, i % 2], acc[i][:].rearrange("p t n -> p n t"))
         warm_up(x_last[1])
 
         hq, hs, e_g = {}, {}, {}
         halves = [slice(0, HALF), slice(HALF, V)]
         e_g[0] = keep.tile([P, HALF], U32, name="e_g0", align_bytes=64)
         e_g[1] = late.tile([P, HALF], U32, name="e_g1", align_bytes=64, offset=4 * S + S)
+        hq_pair = [late.tile([P, HALF], U32, name="hq%d" % g, align_bytes=64, offset=4 * HALF * g) for g in range(2)]
+        hs_pair = [late.tile([P, HALF], U8, name="hs%d" % g, align_bytes=64, offset=4 * S + HALF * g) for g in range(2)]
         for i in range(TILES):
-            hq[i] = late.tile([P, P], U32, name="hq%d" % i, align_bytes=64, offset=4 * P * i)
-            hs[i] = late.tile([P, P], U8, name="hs%d" % i, align_bytes=64, offset=4 * S + P * i)
+            hq[i] = hq_pair[i // 2][:, (i % 2) * P : (i % 2 + 1) * P]
+            hs[i] = hs_pair[i // 2][:, (i % 2) * P : (i % 2 + 1) * P]
 
         def gather_e(half):
             entries = pro_t[:, HALF_COLS * half : HALF_COLS * (half + 1)]
             nc.vector.tensor_copy(e_g[half][:], e_tab[:].bitcast(U32).indirect(entries))
 
-        def quant_h(i):
-            nc.vector.quantize_mx(out=hq[i][:].bitcast(FP8X4), scales=hs[i][:], in_=h_bf[i][:].rearrange("p n t -> p (n t)"))
+        def quant_h(g):
+            nc.vector.quantize_mx(out=hq_pair[g][:].bitcast(FP8X4), scales=hs_pair[g][:], in_=h_bf[g][:].rearrange("p i n t -> p (i n t)"))
 
         def product(i, half, dst):
             nc.tensor.matmul_mx(
                 out=dst,
-                lhsT=hq[i][:].bitcast(FP8X4),
-                lhsT_scale=hs[i][:],
+                lhsT=hq[i].bitcast(FP8X4),
+                lhsT_scale=hs[i],
                 rhs=e_g[half][:].bitcast(FP8X4),
                 rhs_scale=es_p[:, halves[half]],
                 start=True,
@@ -210,8 +213,8 @@ def tile_picked_yphi_soft_p_kernel(tc, x_words, x_scales, w1, e_words, e_scales,
                 out=dst,
                 lhsT=e_g[b // 2][:, (b % 2) * P : (b % 2 + 1) * P].bitcast(FP8X4),
                 lhsT_scale=es_p[:, b * P : (b + 1) * P],
-                rhs=hq[first][:].bitcast(FP8X4),
-                rhs_scale=hs[first][:],
+                rhs=hq[first].bitcast(FP8X4),
+                rhs_scale=hs[first],
                 start=True,
                 stop=True,
             )
@@ -236,7 +239,6 @@ def tile_picked_yphi_soft_p_kernel(tc, x_words, x_scales, w1, e_words, e_scales,
             return ys[i][:, b * P : (b + 1) * P]
 
         quant_h(0)
-        quant_h(1)
         gather_e(1)
         for b in range(2):
             turned(b, 1, scores(1, b))
@@ -244,12 +246,11 @@ def tile_picked_yphi_soft_p_kernel(tc, x_words, x_scales, w1, e_words, e_scales,
             product(0, half, y_first[half][:])
         for b in range(2, blocks):
             turned(b, 1, scores(1, b))
-        quant_h(2)
+        quant_h(1)
         for b in range(blocks):
             turned(b, 2, scores(2, b))
         zs[0] = keep.tile([P, V], F32, name="z0")
         nc.vector.tensor_tensor(zs[0][:, halves[0]], y_first[0][:], inv_b[:, halves[0]], ALU.mult)
-        quant_h(3)
         nc.vector.tensor_tensor(zs[0][:, halves[1]], y_first[1][:], inv_b[:, halves[1]], ALU.mult)
         for b in range(blocks):
             turned(b, 3, scores(3, b))

@@ -22,7 +22,8 @@ K_PASS = P * PACK
 PASSES = K // K_PASS
 TILES = S // P
 HALF = 256
-HALF_COLS = HALF // 16
+BLOCKS = V // P
+TILE_COLS = P // 16
 SPLIT = 320
 CAST = 40
 LATE_BYTES = 4096
@@ -35,7 +36,6 @@ def tile_picked_yphi_soft_p_kernel(tc, x_words, x_scales, w1, e_words, e_scales,
     with ExitStack() as ctx:
         keep = ctx.enter_context(tc.tile_pool(name="keep", bufs=1))
         late = ctx.enter_context(tc.tile_pool(name="late", bufs=1))
-        stats = ctx.enter_context(tc.tile_pool(name="stats", bufs=1))
         psum = ctx.enter_context(tc.psum_pool(name="psum", bufs=1))
 
         offs_t = keep.tile([P, S // 16], U16, name="offs_t")
@@ -110,13 +110,13 @@ def tile_picked_yphi_soft_p_kernel(tc, x_words, x_scales, w1, e_words, e_scales,
         nc.vector.tensor_copy(x_first[:], x_tab[0][:].bitcast(U32).indirect(offs_t[:]))
         quant_w(0)
 
-        inv_t = psum.tile([P, V // P, P], F32, name="inv_t", tag="y0")
-        for b in range(V // P):
+        inv_t = psum.tile([P, BLOCKS, P], F32, name="inv_t", tag="y0")
+        for b in range(BLOCKS):
             nc.tensor.transpose(inv_t[:, b, :], inv_g[:, b * P : (b + 1) * P], ident[:])
-        inv_col = keep.tile([P, V // P], F32, name="inv_col", tag="w_raw0", align_bytes=64)
+        inv_col = keep.tile([P, BLOCKS], F32, name="inv_col", tag="w_raw0", align_bytes=64)
         nc.scalar.copy(inv_col[:], inv_t[:, :, P - 1])
         spread = psum.tile([P, V], F32, name="spread", tag="y1")
-        for b in range(V // P):
+        for b in range(BLOCKS):
             nc.tensor.transpose(spread[:, b * P : (b + 1) * P], inv_col[:, b : b + 1].to_broadcast([P, P]), ident[:])
         inv_b = keep.tile([P, V], F32, name="inv_b")
         nc.scalar.copy(inv_b[:], spread[:])
@@ -124,18 +124,23 @@ def tile_picked_yphi_soft_p_kernel(tc, x_words, x_scales, w1, e_words, e_scales,
         cast_w(1, nc.scalar.copy, slice(0, CAST))
         cast_w(1, nc.vector.tensor_copy, slice(CAST, P))
         quant_w(1)
-        x_last = [keep.tile([P, HALF], U32, name="x_last%d" % half, align_bytes=64) for half in range(2)]
-        for half in range(2):
-            entries = offs_t[:, HALF_COLS * half : HALF_COLS * (half + 1)]
-            nc.vector.tensor_copy(x_last[half][:], x_tab[1][:].bitcast(U32).indirect(entries))
+        x_last = {}
+        for first, count in ((0, 1), (1, 1), (2, 2)):
+            picked = keep.tile([P, count * P], U32, name="x_last%d" % first, align_bytes=64)
+            entries = offs_t[:, TILE_COLS * first : TILE_COLS * (first + count)]
+            nc.vector.tensor_copy(picked[:], x_tab[1][:].bitcast(U32).indirect(entries))
+            for i in range(count):
+                x_last[first + i] = picked[:, i * P : (i + 1) * P]
 
-        h_bf = [keep.tile([P, 2, P, PACK], BF16, name="h_bf%d" % g, align_bytes=64) for g in range(2)]
+        h_bf = [keep.tile([P, P, PACK], BF16, name="h_bf%d" % i, align_bytes=64) for i in range(2)]
+        h_late = keep.tile([P, 2, P, PACK], BF16, name="h_late", align_bytes=64)
+        h_bf = [h_bf[0][:], h_bf[1][:], h_late[:, 0], h_late[:, 1]]
         acc = [psum.tile([P, PACK, P], F32, name="h%d" % i, tag="h%d" % i) for i in range(TILES)]
 
         def project(i, t, o):
             cols = slice(i * P, (i + 1) * P)
             wc = slice(t * P, (t + 1) * P)
-            words = x_first[:, cols] if o == 0 else x_last[i // 2][:, (i % 2) * P : (i % 2 + 1) * P]
+            words = x_first[:, cols] if o == 0 else x_last[i]
             nc.tensor.matmul_mx(
                 out=acc[i][:, t, :],
                 lhsT=wq[o][:, wc].bitcast(FP8X4),
@@ -149,137 +154,75 @@ def tile_picked_yphi_soft_p_kernel(tc, x_words, x_scales, w1, e_words, e_scales,
         for i in range(TILES):
             for t in range(PACK):
                 project(i, t, 0)
-        idle = psum.tile([P, S], F32, name="idle", tag="y3")
-
-        def warm_up(words):
-            nc.tensor.matmul_mx(
-                out=idle[:],
-                lhsT=words[:, :P].bitcast(FP8X4),
-                lhsT_scale=ws[1][:, :P],
-                rhs=x_first[:].bitcast(FP8X4),
-                rhs_scale=xs_p[:],
-                start=True,
-                stop=True,
-            )
-
-        warm_up(wq[1])
         for i in range(TILES):
             for t in range(PACK):
                 project(i, t, 1)
-            copy = nc.vector.tensor_copy if i == 0 else nc.scalar.copy
-            copy(h_bf[i // 2][:, i % 2], acc[i][:].rearrange("p t n -> p n t"))
-        warm_up(x_last[1])
+            nc.scalar.copy(h_bf[i], acc[i][:].rearrange("p t n -> p n t"))
 
-        hq, hs, e_g = {}, {}, {}
+        hq = [keep.tile([P, P], U32, name="hq0", align_bytes=64), late.tile([P, P], U32, name="hq1", align_bytes=64, offset=0)]
+        hs = [keep.tile([P, P], U8, name="hs0", align_bytes=64), late.tile([P, P], U8, name="hs1", align_bytes=64, offset=4 * P)]
+        hq_late = late.tile([P, HALF], U32, name="hq_late", align_bytes=64, offset=8 * HALF)
+        hs_late = late.tile([P, HALF], U8, name="hs_late", align_bytes=64, offset=12 * HALF)
+        e_g = [keep.tile([P, HALF], U32, name="e_g0", align_bytes=64), late.tile([P, HALF], U32, name="e_g1", align_bytes=64, offset=4 * HALF)]
         halves = [slice(0, HALF), slice(HALF, V)]
-        e_g[0] = keep.tile([P, HALF], U32, name="e_g0", align_bytes=64)
-        e_g[1] = late.tile([P, HALF], U32, name="e_g1", align_bytes=64, offset=4 * S + S)
-        hq_pair = [late.tile([P, HALF], U32, name="hq%d" % g, align_bytes=64, offset=4 * HALF * g) for g in range(2)]
-        hs_pair = [late.tile([P, HALF], U8, name="hs%d" % g, align_bytes=64, offset=4 * S + HALF * g) for g in range(2)]
-        for i in range(TILES):
-            hq[i] = hq_pair[i // 2][:, (i % 2) * P : (i % 2 + 1) * P]
-            hs[i] = hs_pair[i // 2][:, (i % 2) * P : (i % 2 + 1) * P]
+
+        def quant_h(i):
+            nc.vector.quantize_mx(out=hq[i][:].bitcast(FP8X4), scales=hs[i][:], in_=h_bf[i].rearrange("p n t -> p (n t)"))
 
         def gather_e(half):
-            entries = pro_t[:, HALF_COLS * half : HALF_COLS * (half + 1)]
+            entries = pro_t[:, 2 * TILE_COLS * half : 2 * TILE_COLS * (half + 1)]
             nc.vector.tensor_copy(e_g[half][:], e_tab[:].bitcast(U32).indirect(entries))
 
-        def quant_h(g):
-            nc.vector.quantize_mx(out=hq_pair[g][:].bitcast(FP8X4), scales=hs_pair[g][:], in_=h_bf[g][:].rearrange("p i n t -> p (i n t)"))
-
-        def product(i, half, dst):
-            nc.tensor.matmul_mx(
-                out=dst,
-                lhsT=hq[i].bitcast(FP8X4),
-                lhsT_scale=hs[i],
-                rhs=e_g[half][:].bitcast(FP8X4),
-                rhs_scale=es_p[:, halves[half]],
-                start=True,
-                stop=True,
-            )
-
-        blocks = V // P
-        ys = {3: psum.tile([P, V], F32, name="y3", tag="y3")}
-        y_second = [psum.tile([P, HALF], F32, name="y1_%d" % half, tag=("y1", "h3")[half]) for half in range(2)]
-        y_shared = [psum.tile([P, HALF], F32, name="y2_%d" % half, tag=("y2", "h2")[half]) for half in range(2)]
-        y_first = [psum.tile([P, HALF], F32, name="y0_%d" % half, tag=("y0", "h0")[half]) for half in range(2)]
-        pair = keep.tile([P, 2, P], F32, name="z_turned_pair")
-        z_turned = {(i, b): keep.tile([P, P], F32, name="z_turned%d_%d" % (i, b))[:] for i in (1, 2, 3) for b in range(blocks) if i != 2 or b > 1}
-        z_turned[2, 0], z_turned[2, 1] = pair[:, 0, :], pair[:, 1, :]
-        zs, total, ex, recip = {}, {}, {}, {}
-
-        def turned(b, first, dst):
-            nc.tensor.matmul_mx(
-                out=dst,
-                lhsT=e_g[b // 2][:, (b % 2) * P : (b % 2 + 1) * P].bitcast(FP8X4),
-                lhsT_scale=es_p[:, b * P : (b + 1) * P],
-                rhs=hq[first].bitcast(FP8X4),
-                rhs_scale=hs[first],
-                start=True,
-                stop=True,
-            )
-
-        def scale_turned(b, dst, src):
-            nc.scalar.activation(dst, src, ACT.Copy, scale=inv_col[:, b : b + 1])
-
-        def turn_back(i, b, src):
-            nc.tensor.transpose(zs[i][:, b * P : (b + 1) * P], src, ident[:])
-
-        def plain(i):
-            zs[i] = keep.tile([P, V], F32, name="z%d" % i)
-            nc.vector.tensor_tensor(zs[i][:], ys[i][:], inv_b[:], ALU.mult)
-
-        gather_e(0)
-        warm_up(e_g[0])
-        def scores(i, b):
-            if i == 2:
-                return y_shared[b // 2][:, (b % 2) * P : (b % 2 + 1) * P]
-            if i == 1:
-                return y_second[b // 2][:, (b % 2) * P : (b % 2 + 1) * P]
-            return ys[i][:, b * P : (b + 1) * P]
-
         quant_h(0)
-        gather_e(1)
-        for b in range(2):
-            turned(b, 1, scores(1, b))
-        for half in range(2):
-            product(0, half, y_first[half][:])
-        for b in range(2, blocks):
-            turned(b, 1, scores(1, b))
+        gather_e(0)
         quant_h(1)
-        for b in range(blocks):
-            turned(b, 2, scores(2, b))
-        zs[0] = keep.tile([P, V], F32, name="z0")
-        nc.vector.tensor_tensor(zs[0][:, halves[0]], y_first[0][:], inv_b[:, halves[0]], ALU.mult)
-        nc.vector.tensor_tensor(zs[0][:, halves[1]], y_first[1][:], inv_b[:, halves[1]], ALU.mult)
-        for b in range(blocks):
-            turned(b, 3, scores(3, b))
-        def turn(i):
-            zs[i] = psum.tile([P, V], F32, name="z%d" % i, tag={1: "h1", 2: "h3", 3: "y0"}[i])
-            for b in range(blocks):
-                if (i, b) == (2, 0):
-                    factors = inv_col[:, 0:2].unsqueeze(2).to_broadcast([P, 2, P])
-                    nc.vector.tensor_tensor(pair[:], y_shared[0][:].rearrange("p (b n) -> p b n", b=2), factors, ALU.mult)
-                elif (i, b) != (2, 1):
-                    scale_turned(b, z_turned[i, b], scores(i, b))
-            for b in range(blocks):
-                turn_back(i, b, z_turned[i, b])
+        gather_e(1)
+        nc.vector.quantize_mx(out=hq_late[:].bitcast(FP8X4), scales=hs_late[:], in_=h_late[:].rearrange("p i n t -> p (i n t)"))
 
-        neg_max = {}
+        scores, turned, zs = {}, {}, {}
+        y_plain = [psum.tile([P, HALF], F32, name="y_plain%d" % half, tag=("y2", "h0")[half]) for half in range(2)]
+        y_first = [psum.tile([P, HALF], F32, name="y_first%d" % half, tag=("y0", "y1")[half]) for half in range(2)]
 
-        def row_max(i):
-            width, place_at = {0: (8, 0), 1: (8, 32), 2: (8, 64), 3: (8, 0)}[i]
-            neg_max[i] = stats.tile([P, width], F32, name="neg_max%d" % i, offset=place_at)[:, 0:1]
-            nc.vector.tensor_reduce(neg_max[i], zs[i][:], AX.X, ALU.max, negate=True)
+        def product(dst, lhs, lhs_scale, rhs, rhs_scale):
+            nc.tensor.matmul_mx(
+                out=dst,
+                lhsT=lhs.bitcast(FP8X4),
+                lhsT_scale=lhs_scale,
+                rhs=rhs.bitcast(FP8X4),
+                rhs_scale=rhs_scale,
+                start=True,
+                stop=True,
+            )
 
-        def exp(i):
-            total[i] = keep.tile([P, 1], F32, name="total%d" % i)
-            ex[i] = keep.tile([P, V], F32, name="ex%d" % i)
-            nc.scalar.activation(ex[i][:], zs[i][:], ACT.Exp, bias=neg_max[i], accum_out=total[i][:])
+        def plain(half):
+            product(y_plain[half][:], hq[1][:], hs[1][:], e_g[half][:], es_p[:, halves[half]])
+
+        codes = {0: (hq[0][:], hs[0][:]), 2: (hq_late[:, :P], hs_late[:, :P]), 3: (hq_late[:, P:], hs_late[:, P:]), 23: (hq_late[:], hs_late[:])}
+
+        def turn(b, who, dst):
+            scores[b, who] = dst
+            product(dst, e_g[b // 2][:, (b % 2) * P : (b % 2 + 1) * P], es_p[:, b * P : (b + 1) * P], *codes[who])
+
+        def scale(b, who):
+            tiles = (2, 3) if who == 23 else (who,)
+            scaled = keep.tile([P, len(tiles), P], F32, name="turned%d_%d" % (b, who))
+            nc.scalar.activation(scaled[:].rearrange("p i n -> p (i n)"), scores[b, who], ACT.Copy, scale=inv_col[:, b : b + 1])
+            for n, i in enumerate(tiles):
+                turned[i, b] = scaled[:, n, :]
+
+        def turn_back(i):
+            zs[i] = psum.tile([P, V], F32, name="z%d" % i, tag={0: "y0", 2: "y2", 3: "y1"}[i])
+            for b in range(BLOCKS):
+                nc.tensor.transpose(zs[i][:, b * P : (b + 1) * P], turned[i, b], ident[:])
+
+        neg_max, total, ex, recip = {}, {}, {}, {}
 
         def exps(i):
-            row_max(i)
-            exp(i)
+            neg_max[i] = keep.tile([P, 1], F32, name="neg_max%d" % i, tag="neg_max%d" % (i % 2 or i + 2))
+            nc.vector.tensor_reduce(neg_max[i][:], zs[i][:], AX.X, ALU.max, negate=True)
+            total[i] = keep.tile([P, 1], F32, name="total%d" % i)
+            ex[i] = keep.tile([P, V], F32, name="ex%d" % i)
+            nc.scalar.activation(ex[i][:], zs[i][:], ACT.Exp, bias=neg_max[i][:], accum_out=total[i][:])
 
         def invert(i):
             recip[i] = keep.tile([P, 1], F32, name="recip%d" % i)
@@ -296,20 +239,44 @@ def tile_picked_yphi_soft_p_kernel(tc, x_words, x_scales, w1, e_words, e_scales,
             queue = nc.scalar if engine == "scalar" else nc.sync
             queue.dma_start(out[i * P : (i + 1) * P, cols], part[:])
 
+        for b in range(2):
+            turn(b, 0, y_first[0][:, b * P : (b + 1) * P])
+        for half in range(2):
+            plain(half)
+        for b in range(2):
+            turn(2 + b, 0, y_first[1][:, b * P : (b + 1) * P])
+        for b in range(BLOCKS):
+            scale(b, 0)
+        zs[1] = keep.tile([P, V], F32, name="z1")
+        for half in range(2):
+            nc.vector.tensor_tensor(zs[1][:, halves[half]], y_plain[half][:], inv_b[:, halves[half]], ALU.mult)
+        y_early = {i: psum.tile([P, 2, P], F32, name="y_early%d" % i, tag="h%d" % i) for i in (2, 3)}
+        for b in range(2):
+            turn(b, 2, y_early[2][:, b, :])
+        for b in (2, 3):
+            turn(b, 23, psum.tile([P, HALF], F32, name="y_wide%d" % b, tag={2: "y3", 3: "h1"}[b])[:])
+        for b in range(2):
+            turn(b, 3, y_early[3][:, b, :])
+        for b in (2, 3):
+            scale(b, 23)
+        pair = keep.tile([P, 2, P], F32, name="pair")
+        nc.vector.tensor_tensor(pair[:], y_early[2][:], inv_col[:, 0:2].unsqueeze(2).to_broadcast([P, 2, P]), ALU.mult)
+        for b in range(2):
+            turned[2, b] = pair[:, b, :]
+            scale(b, 3)
+        for i in (0, 2, 3):
+            turn_back(i)
+
         whole = slice(0, V)
-        turn(1)
-        turn(2)
-        row_max(0)
-        turn(3)
-        exp(0)
         exps(1)
+        exps(0)
         exps(2)
-        invert(0)
-        finish(0, halves[1], "gpsimd")
-        exps(3)
         invert(1)
-        finish(0, halves[0], "vector")
-        finish(1, whole, "vector")
+        finish(1, halves[1], "gpsimd")
+        exps(3)
+        invert(0)
+        finish(1, halves[0], "vector")
+        finish(0, whole, "vector")
         invert(2)
         finish(2, whole, "vector")
         invert(3)

@@ -24,7 +24,7 @@ TILES = S // P
 HALF = 256
 BLOCKS = V // P
 TILE_COLS = P // 16
-SPLIT = 320
+SPLIT = 256
 CAST = 40
 LATE_BYTES = 4096
 
@@ -163,14 +163,15 @@ def tile_picked_yphi_soft_p_kernel(tc, x_words, x_scales, w1, e_words, e_scales,
         hs = [keep.tile([P, P], U8, name="hs0", align_bytes=64), late.tile([P, P], U8, name="hs1", align_bytes=64, offset=4 * P)]
         hq_late = late.tile([P, HALF], U32, name="hq_late", align_bytes=64, offset=8 * HALF)
         hs_late = late.tile([P, HALF], U8, name="hs_late", align_bytes=64, offset=12 * HALF)
-        e_g = [keep.tile([P, HALF], U32, name="e_g0", align_bytes=64), late.tile([P, HALF], U32, name="e_g1", align_bytes=64, offset=4 * HALF)]
+        e_g = [keep.tile([P, 3 * P], U32, name="e_g0", align_bytes=64), late.tile([P, P], U32, name="e_g1", align_bytes=64, offset=4 * HALF)]
+        parts = [slice(0, 3 * P), slice(3 * P, V)]
         halves = [slice(0, HALF), slice(HALF, V)]
 
         def quant_h(i):
             nc.vector.quantize_mx(out=hq[i][:].bitcast(FP8X4), scales=hs[i][:], in_=h_bf[i].rearrange("p n t -> p (n t)"))
 
         def gather_e(half):
-            entries = pro_t[:, 2 * TILE_COLS * half : 2 * TILE_COLS * (half + 1)]
+            entries = pro_t[:, parts[half].start // 16 : parts[half].stop // 16]
             nc.vector.tensor_copy(e_g[half][:], e_tab[:].bitcast(U32).indirect(entries))
 
         quant_h(0)
@@ -180,8 +181,8 @@ def tile_picked_yphi_soft_p_kernel(tc, x_words, x_scales, w1, e_words, e_scales,
         nc.vector.quantize_mx(out=hq_late[:].bitcast(FP8X4), scales=hs_late[:], in_=h_late[:].rearrange("p i n t -> p (i n t)"))
 
         scores, turned, zs = {}, {}, {}
-        y_plain = [psum.tile([P, HALF], F32, name="y_plain%d" % half, tag=("y2", "h0")[half]) for half in range(2)]
-        y_first = [psum.tile([P, HALF], F32, name="y_first%d" % half, tag=("y0", "y1")[half]) for half in range(2)]
+        y_plain = [psum.tile([P, (3 * P, P)[half]], F32, name="y_plain%d" % half, tag=("y2", "h0")[half]) for half in range(2)]
+        y_first = [psum.tile([P, (3 * P, P)[half]], F32, name="y_first%d" % half, tag=("y0", "y1")[half]) for half in range(2)]
 
         def product(dst, lhs, lhs_scale, rhs, rhs_scale):
             nc.tensor.matmul_mx(
@@ -195,13 +196,17 @@ def tile_picked_yphi_soft_p_kernel(tc, x_words, x_scales, w1, e_words, e_scales,
             )
 
         def plain(half):
-            product(y_plain[half][:], hq[1][:], hs[1][:], e_g[half][:], es_p[:, halves[half]])
+            if half == 0:
+                product(y_plain[0][:, :HALF], hq[1][:], hs[1][:], e_g[0][:, :HALF], es_p[:, :HALF])
+                product(y_plain[0][:, HALF:], hq[1][:], hs[1][:], e_g[0][:, HALF:], es_p[:, HALF : 3 * P])
+            else:
+                product(y_plain[1][:], hq[1][:], hs[1][:], e_g[1][:], es_p[:, 3 * P :])
 
         codes = {0: (hq[0][:], hs[0][:]), 2: (hq_late[:, :P], hs_late[:, :P]), 3: (hq_late[:, P:], hs_late[:, P:]), 23: (hq_late[:], hs_late[:])}
 
         def turn(b, who, dst):
             scores[b, who] = dst
-            product(dst, e_g[b // 2][:, (b % 2) * P : (b % 2 + 1) * P], es_p[:, b * P : (b + 1) * P], *codes[who])
+            product(dst, e_g[b // 3][:, (b % 3) * P : (b % 3 + 1) * P], es_p[:, b * P : (b + 1) * P], *codes[who])
 
         def scale(b, who):
             tiles = (2, 3) if who == 23 else (who,)
@@ -218,7 +223,7 @@ def tile_picked_yphi_soft_p_kernel(tc, x_words, x_scales, w1, e_words, e_scales,
         neg_max, total, ex, recip = {}, {}, {}, {}
 
         def exps(i):
-            neg_max[i] = keep.tile([P, 1], F32, name="neg_max%d" % i, tag="neg_max%d" % (i % 2 or i + 2))
+            neg_max[i] = keep.tile([P, 1], F32, name="neg_max%d" % i, tag="neg_max%d" % (i % 3))
             nc.vector.tensor_reduce(neg_max[i][:], zs[i][:], AX.X, ALU.max, negate=True)
             total[i] = keep.tile([P, 1], F32, name="total%d" % i)
             ex[i] = keep.tile([P, V], F32, name="ex%d" % i)
@@ -232,24 +237,21 @@ def tile_picked_yphi_soft_p_kernel(tc, x_words, x_scales, w1, e_words, e_scales,
             part = keep.tile([P, cols.stop - cols.start], F32, name="part%d_%d" % (i, cols.start))
             if engine == "vector":
                 nc.vector.tensor_scalar(part[:], ex[i][:, cols], recip[i][:], None, ALU.mult)
-            elif engine == "gpsimd":
-                nc.gpsimd.tensor_scalar(part[:], ex[i][:, cols], recip[i][:], 1.0, ALU.mult, ALU.mult)
             else:
                 nc.scalar.activation(part[:], ex[i][:, cols], ACT.Copy, scale=recip[i][:])
-            queue = nc.scalar if engine == "scalar" else nc.sync
+            queue = nc.scalar if engine == "scalar" and i == TILES - 1 else nc.sync
             queue.dma_start(out[i * P : (i + 1) * P, cols], part[:])
 
-        for b in range(2):
+        for b in range(3):
             turn(b, 0, y_first[0][:, b * P : (b + 1) * P])
-        for half in range(2):
-            plain(half)
-        for b in range(2):
-            turn(2 + b, 0, y_first[1][:, b * P : (b + 1) * P])
+        plain(0)
+        plain(1)
+        turn(3, 0, y_first[1][:])
         for b in range(BLOCKS):
             scale(b, 0)
         zs[1] = keep.tile([P, V], F32, name="z1")
         for half in range(2):
-            nc.vector.tensor_tensor(zs[1][:, halves[half]], y_plain[half][:], inv_b[:, halves[half]], ALU.mult)
+            nc.vector.tensor_tensor(zs[1][:, parts[half]], y_plain[half][:], inv_b[:, parts[half]], ALU.mult)
         y_early = {i: psum.tile([P, 2, P], F32, name="y_early%d" % i, tag="h%d" % i) for i in (2, 3)}
         for b in range(2):
             turn(b, 2, y_early[2][:, b, :])
@@ -272,12 +274,12 @@ def tile_picked_yphi_soft_p_kernel(tc, x_words, x_scales, w1, e_words, e_scales,
         exps(0)
         exps(2)
         invert(1)
-        finish(1, halves[1], "gpsimd")
-        exps(3)
+        finish(1, whole, "vector")
         invert(0)
-        finish(1, halves[0], "vector")
-        finish(0, whole, "vector")
+        finish(0, halves[1], "scalar")
+        exps(3)
         invert(2)
+        finish(0, halves[0], "vector")
         finish(2, whole, "vector")
         invert(3)
         finish(3, slice(0, SPLIT), "vector")

@@ -46,12 +46,10 @@ def tile_picked_yphi_soft_p_kernel(tc, x_words, x_scales, w1, e_words, e_scales,
         es_tab = keep.tile([P, W], U8, name="es_tab", tag="es_tab", align_bytes=64)
         inv_tab = keep.tile([P, W], F32, name="inv_tab")
         ident = keep.tile([P, P], F32, name="ident")
-        warm = keep.tile([P, 8], F32, name="warm")
 
         nc.gpsimd.memset(xs_tab[0:32, :].bitcast(I32), 0)
         nc.vector.memset(xs_tab[64:P, :].bitcast(I32), 0)
         nc.vector.memset(es_tab[:].bitcast(I32), 0)
-        nc.vector.memset(warm[:], 0.0)
         nc.vector.memset(inv_tab[0 : P - 1, :], 0.0)
         make_identity(nc, ident[:])
 
@@ -64,7 +62,6 @@ def tile_picked_yphi_soft_p_kernel(tc, x_words, x_scales, w1, e_words, e_scales,
 
         nc.scalar.dma_start(xs_tab[32:64, :].bitcast(I32), x_scales.rearrange("o g c -> g o c").bitcast(I32))
         nc.scalar.dma_start(inv_tab[P - 1 : P, :], inv[0:1, :])
-        nc.scalar.activation(warm[:, 1:2], warm[:, 0:1], ACT.Exp)
         nc.sync.dma_start(offs_t[:], offs)
         load_w(0)
         nc.sync.dma_start(pro_t[:], pro)

@@ -236,8 +236,7 @@ def tile_picked_yphi_soft_p_kernel(tc, x_words, x_scales, w1, e_words, e_scales,
                 nc.vector.tensor_scalar(part[:], ex[i][:, cols], recip[i][:], None, ALU.mult)
             else:
                 nc.scalar.activation(part[:], ex[i][:, cols], ACT.Copy, scale=recip[i][:])
-            queue = nc.scalar if engine == "scalar" and i == TILES - 1 else nc.sync
-            queue.dma_start(out[i * P : (i + 1) * P, cols], part[:])
+            return out[i * P : (i + 1) * P, cols], part[:]
 
         for b in range(3):
             turn(b, 0, y_first[0][:, b * P : (b + 1) * P])
@@ -271,13 +270,15 @@ def tile_picked_yphi_soft_p_kernel(tc, x_words, x_scales, w1, e_words, e_scales,
         exps(0)
         exps(2)
         invert(1)
-        finish(1, whole, "vector")
+        nc.sync.dma_start(*finish(1, whole, "vector"))
         invert(0)
-        finish(0, halves[1], "scalar")
+        nc.sync.dma_start(*finish(0, halves[1], "scalar"))
         exps(3)
         invert(2)
-        finish(0, halves[0], "vector")
-        finish(2, whole, "vector")
+        nc.sync.dma_start(*finish(0, halves[0], "vector"))
+        nc.sync.dma_start(*finish(2, whole, "vector"))
         invert(3)
-        finish(3, slice(0, SPLIT), "vector")
-        finish(3, slice(SPLIT, V), "scalar")
+        by_vector = finish(3, slice(0, SPLIT), "vector")
+        by_scalar = finish(3, slice(SPLIT, V), "scalar")
+        nc.scalar.dma_start(*by_vector)
+        nc.sync.dma_start(*by_scalar)

@@ -24,7 +24,7 @@ TILES = S // P
 HALF = 256
 BLOCKS = V // P
 TILE_COLS = P // 16
-SPLIT = 256
+SPLIT = 320
 CAST = 40
 LATE_BYTES = 4096
 

from contextlib import ExitStack

import concourse.mybir as mybir
from concourse.masks import make_identity

F32 = mybir.dt.float32
BF16 = mybir.dt.bfloat16
I32 = mybir.dt.int32
U32 = mybir.dt.uint32
U16 = mybir.dt.uint16
U8 = mybir.dt.uint8
FP8X4 = mybir.dt.float8_e4m3fn_x4
ALU = mybir.AluOpType
ACT = mybir.ActivationFunctionType
AX = mybir.AxisListType

P = 128
K, T, S = 1024, 2048, 512
H, W, V = 512, 2048, 512
PACK = 4
K_PASS = P * PACK
PASSES = K // K_PASS
TILES = S // P
HALF = 256
BLOCKS = V // P
TILE_COLS = P // 16
SPLIT = 320
CAST = 40
LATE_BYTES = 4096

FLOPS = 2 * K * H * S + 2 * H * S * V


def tile_picked_yphi_soft_p_kernel(tc, x_words, x_scales, w1, e_words, e_scales, inv, offs, pro, out):
    nc = tc.nc
    with ExitStack() as ctx:
        keep = ctx.enter_context(tc.tile_pool(name="keep", bufs=1))
        late = ctx.enter_context(tc.tile_pool(name="late", bufs=1))
        psum = ctx.enter_context(tc.psum_pool(name="psum", bufs=1))

        offs_t = keep.tile([P, S // 16], U16, name="offs_t")
        pro_t = keep.tile([P, V // 16], U16, name="pro_t")
        w_raw = [keep.tile([P, PACK, H], F32, name="w_raw%d" % o, tag="w_raw%d" % o, align_bytes=64) for o in range(PASSES)]
        x_tab = {0: keep.tile([P, T], I32, name="x_tab0")}
        xs_tab = keep.tile([P, T], U8, name="xs_tab", tag="xs_tab")
        es_tab = keep.tile([P, W], U8, name="es_tab", tag="es_tab", align_bytes=64)
        inv_tab = keep.tile([P, W], F32, name="inv_tab")
        ident = keep.tile([P, P], F32, name="ident")

        nc.gpsimd.memset(xs_tab[0:32, :].bitcast(I32), 0)
        nc.vector.memset(xs_tab[64:P, :].bitcast(I32), 0)
        nc.vector.memset(es_tab[:].bitcast(I32), 0)
        nc.vector.memset(inv_tab[0 : P - 1, :], 0.0)
        make_identity(nc, ident[:])

        def load_w(o):
            rows = w1[K_PASS * o : K_PASS * (o + 1), :]
            nc.sync.dma_start(w_raw[o][:], rows.rearrange("(p j) c -> p j c", j=PACK))

        def load_x(o):
            nc.sync.dma_start(x_tab[o][:], x_words[o].rearrange("p n t -> p (n t)").bitcast(I32))

        nc.scalar.dma_start(xs_tab[32:64, :].bitcast(I32), x_scales.rearrange("o g c -> g o c").bitcast(I32))
        nc.scalar.dma_start(inv_tab[P - 1 : P, :], inv[0:1, :])
        nc.sync.dma_start(offs_t[:], offs)
        load_w(0)
        nc.sync.dma_start(pro_t[:], pro)
        nc.sync.dma_start(es_tab[32:96:4, :].bitcast(I32), e_scales[0].bitcast(I32))
        load_x(0)
        load_w(1)

        def place(plane, gathered, step):
            for r in range(4):
                nc.sync.dma_start(plane[r:P:4, :].bitcast(I32), gathered[32 + 2 * step * r : 32 + 2 * step * r + 32 * step : step, :].bitcast(I32))

        wq = {}
        ws = [keep.tile([P, H], U8, name="ws%d" % o, align_bytes=64) for o in range(PASSES)]
        w_bf = [keep.tile([P, PACK * H], BF16, name="w_bf%d" % o, align_bytes=64) for o in range(PASSES)]

        def cast_w(o, copy, ms):
            copy(
                w_bf[o][:].rearrange("p (t m j) -> p m j t", t=PACK, j=PACK)[:, ms],
                w_raw[o][:].rearrange("p j (m t) -> p m j t", t=PACK)[:, ms],
            )

        def quant_w(o):
            wq[o] = keep.tile([P, H], U32, name="wq%d" % o, align_bytes=64)
            nc.vector.quantize_mx(out=wq[o][:].bitcast(FP8X4), scales=ws[o][:], in_=w_bf[o][:])

        xs_g = keep.tile([P, S], U8, name="xs_g")
        nc.vector.tensor_copy(xs_g[:], xs_tab[:].indirect(offs_t[:]))
        xs_p = keep.tile([P, S], U8, name="xs_p", align_bytes=64)
        x_tab[1] = keep.tile([P, T], I32, name="x_tab1", tag="xs_tab")
        place(xs_p, xs_g[:], 1)
        load_x(1)
        inv_g = keep.tile([P, V], F32, name="inv_g")
        nc.vector.tensor_copy(inv_g[:], inv_tab[:].indirect(pro_t[:]))
        cast_w(0, nc.scalar.copy, slice(0, P))
        es_g = late.tile([P, LATE_BYTES], U8, name="es_g", align_bytes=64, offset=0)
        nc.vector.tensor_copy(es_g[:, :V], es_tab[:].indirect(pro_t[:]))
        e_tab = keep.tile([P, W], I32, name="e_tab", tag="es_tab", align_bytes=64)
        nc.sync.dma_start(e_tab[:], e_words[0].rearrange("p n t -> p (n t)").bitcast(I32))
        es_p = keep.tile([P, V], U8, name="es_p", align_bytes=64)
        place(es_p, es_g[:, :V], 2)

        x_first = keep.tile([P, S], U32, name="x_first", align_bytes=64)
        nc.vector.tensor_copy(x_first[:], x_tab[0][:].bitcast(U32).indirect(offs_t[:]))
        quant_w(0)

        inv_t = psum.tile([P, BLOCKS, P], F32, name="inv_t", tag="y0")
        for b in range(BLOCKS):
            nc.tensor.transpose(inv_t[:, b, :], inv_g[:, b * P : (b + 1) * P], ident[:])
        inv_col = keep.tile([P, BLOCKS], F32, name="inv_col", tag="w_raw0", align_bytes=64)
        nc.scalar.copy(inv_col[:], inv_t[:, :, P - 1])
        spread = psum.tile([P, V], F32, name="spread", tag="y1")
        for b in range(BLOCKS):
            nc.tensor.transpose(spread[:, b * P : (b + 1) * P], inv_col[:, b : b + 1].to_broadcast([P, P]), ident[:])
        inv_b = keep.tile([P, V], F32, name="inv_b")
        nc.scalar.copy(inv_b[:], spread[:])

        cast_w(1, nc.scalar.copy, slice(0, CAST))
        cast_w(1, nc.vector.tensor_copy, slice(CAST, P))
        quant_w(1)
        x_last = {}
        for first, count in ((0, 1), (1, 1), (2, 2)):
            picked = keep.tile([P, count * P], U32, name="x_last%d" % first, align_bytes=64)
            entries = offs_t[:, TILE_COLS * first : TILE_COLS * (first + count)]
            nc.vector.tensor_copy(picked[:], x_tab[1][:].bitcast(U32).indirect(entries))
            for i in range(count):
                x_last[first + i] = picked[:, i * P : (i + 1) * P]

        h_bf = [keep.tile([P, P, PACK], BF16, name="h_bf%d" % i, align_bytes=64) for i in range(2)]
        h_late = keep.tile([P, 2, P, PACK], BF16, name="h_late", align_bytes=64)
        h_bf = [h_bf[0][:], h_bf[1][:], h_late[:, 0], h_late[:, 1]]
        acc = [psum.tile([P, PACK, P], F32, name="h%d" % i, tag="h%d" % i) for i in range(TILES)]

        def project(i, t, o):
            cols = slice(i * P, (i + 1) * P)
            wc = slice(t * P, (t + 1) * P)
            words = x_first[:, cols] if o == 0 else x_last[i]
            nc.tensor.matmul_mx(
                out=acc[i][:, t, :],
                lhsT=wq[o][:, wc].bitcast(FP8X4),
                lhsT_scale=ws[o][:, wc],
                rhs=words.bitcast(FP8X4),
                rhs_scale=xs_p[4 * o : P, cols],
                start=(o == 0 and t == 0),
                stop=(o == PASSES - 1 and t == PACK - 1),
            )

        for i in range(TILES):
            for t in range(PACK):
                project(i, t, 0)
        for i in range(TILES):
            for t in range(PACK):
                project(i, t, 1)
            nc.scalar.copy(h_bf[i], acc[i][:].rearrange("p t n -> p n t"))

        hq = [keep.tile([P, P], U32, name="hq0", align_bytes=64), late.tile([P, P], U32, name="hq1", align_bytes=64, offset=0)]
        hs = [keep.tile([P, P], U8, name="hs0", align_bytes=64), late.tile([P, P], U8, name="hs1", align_bytes=64, offset=4 * P)]
        hq_late = late.tile([P, HALF], U32, name="hq_late", align_bytes=64, offset=8 * HALF)
        hs_late = late.tile([P, HALF], U8, name="hs_late", align_bytes=64, offset=12 * HALF)
        e_g = [keep.tile([P, 3 * P], U32, name="e_g0", align_bytes=64), late.tile([P, P], U32, name="e_g1", align_bytes=64, offset=4 * HALF)]
        parts = [slice(0, 3 * P), slice(3 * P, V)]
        halves = [slice(0, HALF), slice(HALF, V)]

        def quant_h(i):
            nc.vector.quantize_mx(out=hq[i][:].bitcast(FP8X4), scales=hs[i][:], in_=h_bf[i].rearrange("p n t -> p (n t)"))

        def gather_e(half):
            entries = pro_t[:, parts[half].start // 16 : parts[half].stop // 16]
            nc.vector.tensor_copy(e_g[half][:], e_tab[:].bitcast(U32).indirect(entries))

        quant_h(0)
        gather_e(0)
        quant_h(1)
        gather_e(1)
        nc.vector.quantize_mx(out=hq_late[:].bitcast(FP8X4), scales=hs_late[:], in_=h_late[:].rearrange("p i n t -> p (i n t)"))

        scores, turned, zs = {}, {}, {}
        y_plain = [psum.tile([P, (3 * P, P)[half]], F32, name="y_plain%d" % half, tag=("y2", "h0")[half]) for half in range(2)]
        y_first = [psum.tile([P, (3 * P, P)[half]], F32, name="y_first%d" % half, tag=("y0", "y1")[half]) for half in range(2)]

        def product(dst, lhs, lhs_scale, rhs, rhs_scale):
            nc.tensor.matmul_mx(
                out=dst,
                lhsT=lhs.bitcast(FP8X4),
                lhsT_scale=lhs_scale,
                rhs=rhs.bitcast(FP8X4),
                rhs_scale=rhs_scale,
                start=True,
                stop=True,
            )

        def plain(half):
            if half == 0:
                product(y_plain[0][:, :HALF], hq[1][:], hs[1][:], e_g[0][:, :HALF], es_p[:, :HALF])
                product(y_plain[0][:, HALF:], hq[1][:], hs[1][:], e_g[0][:, HALF:], es_p[:, HALF : 3 * P])
            else:
                product(y_plain[1][:], hq[1][:], hs[1][:], e_g[1][:], es_p[:, 3 * P :])

        codes = {0: (hq[0][:], hs[0][:]), 2: (hq_late[:, :P], hs_late[:, :P]), 3: (hq_late[:, P:], hs_late[:, P:]), 23: (hq_late[:], hs_late[:])}

        def turn(b, who, dst):
            scores[b, who] = dst
            product(dst, e_g[b // 3][:, (b % 3) * P : (b % 3 + 1) * P], es_p[:, b * P : (b + 1) * P], *codes[who])

        def scale(b, who):
            tiles = (2, 3) if who == 23 else (who,)
            scaled = keep.tile([P, len(tiles), P], F32, name="turned%d_%d" % (b, who))
            nc.scalar.activation(scaled[:].rearrange("p i n -> p (i n)"), scores[b, who], ACT.Copy, scale=inv_col[:, b : b + 1])
            for n, i in enumerate(tiles):
                turned[i, b] = scaled[:, n, :]

        def turn_back(i):
            zs[i] = psum.tile([P, V], F32, name="z%d" % i, tag={0: "y0", 2: "y2", 3: "y1"}[i])
            for b in range(BLOCKS):
                nc.tensor.transpose(zs[i][:, b * P : (b + 1) * P], turned[i, b], ident[:])

        neg_max, total, ex, recip = {}, {}, {}, {}

        def exps(i):
            neg_max[i] = keep.tile([P, 1], F32, name="neg_max%d" % i, tag="neg_max%d" % (i % 3))
            nc.vector.tensor_reduce(neg_max[i][:], zs[i][:], AX.X, ALU.max, negate=True)
            total[i] = keep.tile([P, 1], F32, name="total%d" % i)
            ex[i] = keep.tile([P, V], F32, name="ex%d" % i)
            nc.scalar.activation(ex[i][:], zs[i][:], ACT.Exp, bias=neg_max[i][:], accum_out=total[i][:])

        def invert(i):
            recip[i] = keep.tile([P, 1], F32, name="recip%d" % i)
            nc.vector.reciprocal(recip[i][:], total[i][:])

        def finish(i, cols, engine):
            part = keep.tile([P, cols.stop - cols.start], F32, name="part%d_%d" % (i, cols.start))
            if engine == "vector":
                nc.vector.tensor_scalar(part[:], ex[i][:, cols], recip[i][:], None, ALU.mult)
            else:
                nc.scalar.activation(part[:], ex[i][:, cols], ACT.Copy, scale=recip[i][:])
            return out[i * P : (i + 1) * P, cols], part[:]

        for b in range(3):
            turn(b, 0, y_first[0][:, b * P : (b + 1) * P])
        plain(0)
        plain(1)
        turn(3, 0, y_first[1][:])
        for b in range(BLOCKS):
            scale(b, 0)
        zs[1] = keep.tile([P, V], F32, name="z1")
        for half in range(2):
            nc.vector.tensor_tensor(zs[1][:, parts[half]], y_plain[half][:], inv_b[:, parts[half]], ALU.mult)
        y_early = {i: psum.tile([P, 2, P], F32, name="y_early%d" % i, tag="h%d" % i) for i in (2, 3)}
        for b in range(2):
            turn(b, 2, y_early[2][:, b, :])
        for b in (2, 3):
            turn(b, 23, psum.tile([P, HALF], F32, name="y_wide%d" % b, tag={2: "y3", 3: "h1"}[b])[:])
        for b in range(2):
            turn(b, 3, y_early[3][:, b, :])
        for b in (2, 3):
            scale(b, 23)
        pair = keep.tile([P, 2, P], F32, name="pair")
        nc.vector.tensor_tensor(pair[:], y_early[2][:], inv_col[:, 0:2].unsqueeze(2).to_broadcast([P, 2, P]), ALU.mult)
        for b in range(2):
            turned[2, b] = pair[:, b, :]
            scale(b, 3)
        for i in (0, 2, 3):
            turn_back(i)

        whole = slice(0, V)
        exps(1)
        exps(0)
        exps(2)
        invert(1)
        nc.sync.dma_start(*finish(1, whole, "vector"))
        invert(0)
        nc.sync.dma_start(*finish(0, halves[1], "scalar"))
        exps(3)
        invert(2)
        nc.sync.dma_start(*finish(0, halves[0], "vector"))
        nc.sync.dma_start(*finish(2, whole, "vector"))
        invert(3)
        by_vector = finish(3, slice(0, SPLIT), "vector")
        by_scalar = finish(3, slice(SPLIT, V), "scalar")
        nc.scalar.dma_start(*by_vector)
        nc.sync.dma_start(*by_scalar)
